import numpy as np, ml_dtypes
CORES = [16,17,18,19,32,33,34,35]
N = 8
import mx_ref
BF = ml_dtypes.bfloat16
def gentries(a):
    return np.ascontiguousarray(a.reshape(8, 16, -1).transpose(0, 2, 1)).reshape(8, -1)
def gtable(e):
    e = np.asarray(e); return np.ascontiguousarray(e.reshape(8, -1, 16).transpose(0, 2, 1)).reshape(128, -1).astype(np.int32)
def gcols(t, e):
    v = np.concatenate([t.reshape(8, 16, -1, 4), np.zeros((8, 16, 1, 4), BF)], axis=2)
    return np.ascontiguousarray(np.stack([v[g][:, e[g]] for g in range(8)])).reshape(128, -1)
def tile(rs):
    return np.stack(rs, axis=2).reshape(128, -1).astype(BF)
def pick(q, e):
    c = np.concatenate([q[0].reshape(128, -1, 4), np.zeros((128, 1, 4), np.uint8)], axis=1); s = np.concatenate([q[1], np.ones((16, 1), np.uint8)], axis=1)
    return (np.ascontiguousarray(c[:, e].reshape(128, -1)), np.ascontiguousarray(s[:, e]))
def join(*qs):
    return (np.concatenate([q[0] for q in qs], axis=1), np.concatenate([q[1] for q in qs], axis=1))
def put(q, e, v):
    c, s = q[0].reshape(128, -1, 4).copy(), q[1].copy(); c[:, e] = v[0].reshape(128, -1, 4); s[:, e] = v[1]
    return (c.reshape(128, -1), s)
def pk(c, s):
    return (np.ascontiguousarray(c), mx_ref.live(s))
def emit(q):
    return q[0], q[1]
def packed(v, rng):
    q = [mx_ref.quantize(np.ascontiguousarray(v[r])) for r in range(N)]
    return np.stack([a for a, b in q]), np.stack([mx_ref.plane(b, rng) for a, b in q])
def values_of_codes():
    e, c = np.zeros((128, 128, 4), np.float32), np.zeros((128, 2, 4), np.uint8)
    e[np.arange(128), np.arange(128), 0] = 1
    c[:127, :, 0] = np.arange(256).reshape(2, 128).T[:127]
    return mx_ref.matmul(mx_ref.quantize(e.reshape(128, 512).astype(BF)), (c.reshape(128, 8), np.full((16, 2), 127, np.uint8))).T.reshape(-1).astype(np.float64)
CODE_VALUE, SCALE_VALUE = values_of_codes(), 2.0 ** (np.arange(256) - 127.0)
def decode(q):
    return (CODE_VALUE[q[0]].reshape(16, 8, -1, 4) * SCALE_VALUE[q[1]][:, None, :, None] + 0.0).reshape(128, -1).astype(np.float32)
def f(rng, *shape):
    return mx_ref.flush((rng.standard_normal(shape, dtype=np.float32) * np.exp2(rng.integers(-2, 3, shape[:-1] + (1,)))).astype(BF))
def wide(rng, *shape, cols=0):
    v = rng.standard_normal(shape, dtype=np.float32) * np.exp2(rng.integers(-12, 13, shape)).astype(np.float32)
    if cols: v *= np.repeat(np.exp2(rng.integers(-cols, cols + 1, shape[:-2] + (1, shape[-1] // 4))) * (rng.random(shape[:-2] + (1, shape[-1] // 4)) > 0.0625), 4, axis=-1).astype(np.float32)
    return mx_ref.flush(v.astype(BF))
C = 320
STEP = [1, 2, 4]
GAPS = [[2, 4, 5, 6, 7, 8], [3, 4, 5, 6, 7, 8]]
def numbers_of(rng):
    return {"x": np.array(f(rng, N, 128, 4 * C)), "u": np.array(f(rng, N, 128, 512)), "v": np.array(f(rng, N, 128, 512))}
def full(rng, k):
    h = 128 + rng.permutation(128)[:k]
    low = rng.permutation(np.concatenate([2 * h, 2 * h + 1]))[:C - 127 - k]
    return np.sort(np.concatenate([np.arange(1, 128), h, low]))
def below(h):
    return np.concatenate([np.arange(h << n, (h + 1) << n) for n in range(10 - h.bit_length())])
def lean(side, slot):
    c = 3 - side
    return np.sort(np.concatenate([[1], below(2 + side), np.concatenate([[c], below(2 * c + slot)])[:C - 256]]))
def ragged(rng, first):
    cuts, left = [], 511 - C
    for n, most in [(n, 1) for n in first] + [(n, 9) for n in range(3, 9)]:
        size = 2 ** (9 - n) - 1
        k = min(most, left // size)
        cuts += [n] * k
        left -= k * size
    keep = np.arange(512) > 0
    for n in sorted(cuts):
        h = np.arange(2 ** n, 2 ** (n + 1))
        h = int(rng.choice(h[keep[h] & keep[h ^ 1]]))
        keep[below(h)] = False
    return np.flatnonzero(keep)
def grown(h, places):
    at = np.zeros(512, np.int64)
    at[h] = places
    e = np.zeros(C, np.int64)
    e[places[1:]] = 2 * at[h[1:] >> 1] + (h[1:] & 1)
    return e
def shuffled(rng):
    return np.concatenate([[0], 1 + rng.permutation(C - 1)])
def trees(rng):
    t = np.stack([np.stack([grown(full(rng, int(rng.integers(112, 129))), shuffled(rng)) for g in range(8)]) for r in range(N)])
    o = rng.permutation(8)
    for r in range(N):
        for n in range(2): t[r, o[(r + 4 * n) % 8]] = grown(ragged(rng, GAPS[n]), shuffled(rng))
    return t
def stored(t):
    return {"se": np.stack([gtable(t[r]) for r in range(N)])}
def weights(rng, w):
    c, s = packed(np.ascontiguousarray(w).reshape(N, 128, 2048), rng)
    return {"wc": c, "ws": s}
def layers(rng, still=[], pairs=False):
    w = np.array(f(rng, N, 128, 2048)).reshape(N, 8, 16, 4, 8, 16, 4)
    for i in still:
        w[:, :, i] = 0
        w[:, :, :, :, :, i] = 0
    if pairs:
        w[:, :, :, :, :, 8:] = 0
        for g in range(8):
            w[:, g, 8, 0, g, 8, 0] = -28.0
            for b in range(4): w[:, g, 10, b, g, 9, 0] = -2.0 ** (b - 5)
    return weights(rng, w)
def setup_inputs(rng):
    return {**numbers_of(rng), **stored(trees(rng)), **layers(rng)}
def setup_inputs_ties(rng):
    d = numbers_of(rng)
    o = rng.permutation(N)
    k = rng.integers(-1, 2, (N, 8, C)).astype(np.float32)
    k[o[1]] = -1
    x = d["x"].reshape(N, 8, 16, C, 4)
    x[:, :, 0] = 0
    x[:, :, 0, :, 0] = k.astype(BF)
    a = np.exp2(rng.integers(-3, 4, (1, 8, 1)).astype(np.float32))
    x[:, :, 8:] = 0
    x[:, :, 8, :, 0] = (-1.125 * a).astype(BF)
    x[:, :, 10, :, 0] = (-0.0703125 * a).astype(BF)
    c = np.ones(N, np.float32)
    c[o[0]] = 0
    c[o[2]] = -1
    u = d["u"].reshape(N, 128, 128, 4)
    u[:, :, ::16] = 0
    for h in range(0, 128, 16): u[:, h, h, 0] = c.astype(BF)
    return {"x": x.reshape(N, 128, 4 * C), "u": u.reshape(N, 128, 512), "v": d["v"], **stored(trees(rng)), **layers(rng, [0], True)}
def setup_inputs_near(rng):
    d = numbers_of(rng)
    o = rng.permutation(N) % 2
    k = np.where(o == 0, 2.0 ** -30, 1.0).astype(np.float32)
    x = np.zeros((N, 8, 16, C, 4), np.float32)
    s = rng.integers(-1, 2, (N, 8, C)) * k[:, None, None]
    x[:, :, 0, :, 0] = 1.125 * s
    x[:, :, 1, :, 0] = -1.25 * s
    s = rng.choice([-1.0, 1.0], (N, 8, C)) * 2.0 ** -30
    x[:, :, 8, :, 0] = 1.125 * s
    x[:, :, 9, :, 0] = -1.25 * s
    x[:, :, 2, :, 0] = 2.0 ** -28
    x[:, :, 10, :, 0] = 2.0 ** -28
    for r in range(N):
        at = [0, C - 1, int(rng.integers(C)), int(rng.integers(C))]
        for g, j in zip(rng.permutation(8)[:4], at): x[r, g, 0, j, 0] = 2.0 ** 30 * rng.choice([-1.0, 1.0])
    u = d["u"].astype(np.float32).reshape(N, 128, 128, 4)
    u[:, :, ::16] = 0
    w = np.zeros((N, 128, 4, 128, 4), np.float32)
    for h in range(0, 128, 16):
        u[:, h, h, 0] = 1.125 * k
        u[:, h + 1, h, 0] = k
        w[:, h + 8, 0, h, 0] = 0.5
        w[:, h + 9, 0, h + 1, 0] = 0.5
        w[:, h + 10, 0, h + 2, 0] = 32.0
        w[:, h + 10, 0, h + 10, 0] = 32.0
    return {"x": x.reshape(N, 128, 4 * C).astype(BF), "u": u.reshape(N, 128, 512).astype(BF), "v": d["v"], **stored(trees(rng)), **weights(rng, w.astype(BF))}
def setup_inputs_odd(rng):
    d = numbers_of(rng)
    x = (1.0 + (2 * rng.integers(0, 64, (N, 16, 8, C, 4)) + 1) * 2.0 ** -7) * np.exp2(-rng.integers(0, 7, (N, 16, 8, C, 4)).astype(np.float64)) * rng.choice([-1.0, 1.0], (N, 16, 8, C, 4))
    x[:, :, 0, :, 0] = 1.96875 * 2.0 ** 8 * rng.choice([-1.0, 1.0], (N, 16, C))
    e = rng.choice([-1.0, 1.0], (N, 8, C)) * 2.0 ** -5
    x[:, ::2, 1, :, 0] = 1.125 * e
    x[:, ::2, 2, :, 0] = -e
    u = d["u"].reshape(N, 128, 128, 4)
    u[:, :, ::16] = 0
    for h in range(0, 128, 16): u[:, h + 1:h + 3, h, 0] = 1
    return {"x": x.astype(np.float32).reshape(N, 128, 4 * C).astype(BF), "u": u.reshape(N, 128, 512), "v": d["v"], **stored(trees(rng)), **layers(rng, [0, 8])}
def setup_inputs_ends(rng):
    d = numbers_of(rng)
    o, e = rng.permutation(N) % 4, rng.permutation(N) % 4
    x = np.zeros((N, 128, C, 4))
    u = d["u"].astype(np.float32).reshape(N, 128, 128, 4)
    v = d["v"].astype(np.float32)
    w = np.zeros((N, 128, 4, 128, 4), np.float32)
    t = np.zeros((N, 8, C), np.int64)
    i = np.arange(128)
    last = i % 16 == 15
    for r in range(N):
        h = rng.permutation(8)
        c = np.where(h < 2, 0.0, h % 2 * 2.0 - 1.0)[None, :, None]
        a = -(0.9 + 0.1 * rng.random((128, C, 4))) * 2.0 ** 30
        if o[r] == 1: a = a * rng.choice([-1.0, 1.0], (C, 1))
        if o[r] == 2: a = -(1.0 + 0.125 * rng.integers(0, 8, (128, C, 4))) * 2.0 ** -30
        if o[r] == 3: a = d["x"][r].astype(np.float32).reshape(128, C, 4)[:, :1]
        x[r] = a
        if o[r] < 2:
            x[r, last] = 2.0 ** -30
            u[r, :, ::16] = c * (0.9 + 0.1 * rng.random((128, 8, 4))) * 2.0 ** 30
            v[r] = rng.choice([-1.0, 1.0], (128, 512)) * (0.9 + 0.1 * rng.random((128, 512))) * 2.0 ** 30
        if o[r] == 2:
            u[r, :, ::16] = c * (1.0 + 0.125 * rng.integers(0, 8, (128, 8, 4))) * 2.0 ** -30
            v[r] = rng.choice([-1.0, 1.0], (128, 512)) * (1.0 + 0.125 * rng.integers(0, 8, (128, 512))) * 2.0 ** -30
        if o[r] == 3: u[r, :, ::16] *= np.abs(c).astype(np.float32)
        k = np.where(last, [32.0, 32.0, 256.0, 2.0 ** -8][o[r]], 32.0)
        for b in range(4): w[r, i, b, i, b] = k
        for g in range(8):
            if e[r] == 0: t[r, g] = grown(lean(0, g % 2), np.arange(C))
            if e[r] == 1: t[r, g] = grown(lean(1, g % 2), np.concatenate([[0], np.arange(C - 1, 0, -1)]))
            if e[r] >= 2: t[r, g] = grown(ragged(rng, GAPS[g - 6]) if g >= 6 else full(rng, 128 if e[r] == 2 else (C - 125) // 3), shuffled(rng))
    return {"x": x.astype(np.float32).reshape(N, 128, 4 * C).astype(BF), "u": u.reshape(N, 128, 512).astype(BF), "v": v.astype(BF), **stored(t), **weights(rng, w.astype(BF))}
def setup_inputs_spread(rng):
    d = setup_inputs(rng)
    d["x"] = wide(rng, N, 128, 4 * C, cols=6)
    return d
def check_inputs(d):
    b = []
    for k in ("x", "u", "v"):
        a = np.abs(d[k].astype(np.float32))
        if not (np.isfinite(a).all() and ((a == 0) | (a >= 2.0 ** -30) & (a <= 2.0 ** 30)).all()): b.append("a value of " + k)
    e = np.stack([gentries(d["se"][r]) for r in range(N)])
    if not ((e >= 0) & (e < 2 * C)).all(): b.append("an entry of se")
    else:
        if e[:, :, 0].any(): b.append("se: entry 0")
        if (np.diff(np.sort(e[:, :, 1:], axis=2), axis=2) == 0).any(): b.append("se: equal seats")
        a = e >> 1
        for n in range(7): a = np.take_along_axis(e >> 1, a, 2)
        if a.any(): b.append("se: a place from which eight steps don't lead to place 0")
    none, least, most = [emit(mx_ref.quantize(np.full((128, 16), k, np.float32).astype(BF)))[1][0, 0] for k in (0.0, 2.0 ** -8, 2.0 ** 8)]
    for r in range(N):
        if ((d["wc"][r] == 0x7F) | (d["wc"][r] == 0xFF)).any(): b.append("wc: a code that is no number")
        s = mx_ref.live(d["ws"][r])
        if ((s != none) & ((s < least) | (s > most))).any(): b.append("ws: a scale out of range")
        if (((d["wc"][r].reshape(16, 8, 512, 4) & 0x7F) != 0) & (s == none)[:, None, :, None]).any(): b.append("wc: a code other than zero under the scale of zeros")
    return b
def reference(x, u, v, se, wc, ws):
    qu = [mx_ref.quantize(u[r]) for r in range(N)]
    lay = [pk(wc[r], ws[r]) for r in range(N)]
    seat = [gentries(se[r]).astype(np.int64) for r in range(N)]
    par = [seat[r] >> 1 for r in range(N)]
    now = [x[r] for r in range(N)]
    y, im = np.zeros((N, 128, C), np.float32), np.zeros((N, 8, C), np.float32)
    oc, osc = np.zeros((N, 128, 4 * C), np.uint8), np.zeros((N, 16, C), np.uint8)
    for step in STEP:
        q = [mx_ref.quantize(now[r]) for r in range(N)]
        layered, child = [], []
        for r in range(N):
            layered.append(tile([mx_ref.matmul(pick(lay[r], np.arange(128 * b, 128 * b + 128)), q[r]) * np.float32(0.03125) for b in range(4)]))
            turn = (mx_ref.matmul(qu[r], q[r])[::16] < 0).astype(np.int64)
            seat[r] = seat[r] ^ np.take_along_axis(turn, par[r], 1)
            c = np.full((8, 2 * C), -1, np.int64)
            np.put_along_axis(c, seat[r][:, 1:], np.tile(np.arange(1, C), (8, 1)), 1)
            child.append(c)
        for r in range(N):
            p = r ^ step
            m = np.zeros((8, C), np.int64)
            for depth in range(8):
                at = np.take_along_axis(m, par[r], 1)
                c = np.take_along_axis(child[p], 2 * at + (seat[r] & 1), 1)
                m = np.where(c < 0, at, c)
                m[:, 0] = 0
            e = mx_ref.quantize(gcols(layered[p], m))
            above = gcols(decode(q[r]).astype(BF), par[r]).astype(np.float32)
            now[r] = ((decode(e) + above) * np.float32(0.5)).astype(BF)
            im[r] = m
    for r in range(N):
        z = mx_ref.quantize(now[r])
        y[r] = mx_ref.matmul(mx_ref.quantize(v[r]), z)
        oc[r], osc[r] = emit(z)
    return {"y": y, "im": im, "oc": oc, "osc": osc}

@@ -1,0 +1,357 @@
+import numpy as np
+from concourse.mybir import dt, AluOpType, AxisListType, ActivationFunctionType
+
+C = 320
+STEP = [1, 2, 4]
+A = AluOpType
+COPY = ActivationFunctionType.Copy
+
+SCRATCH = {
+    "ps": ("psum", [128, 4096], "float32"),
+    "x0": ("sbuf", [128, 1280], "bfloat16"), "ub": ("sbuf", [128, 512], "bfloat16"), "vb": ("sbuf", [128, 512], "bfloat16"),
+    "uq": ("sbuf", [128, 128], "float8_e4m3fn_x4"), "us": ("sbuf", [128, 128], "uint8"),
+    "ur": ("sbuf", [128, 128], "float8_e4m3fn_x4"), "urs": ("sbuf", [128, 128], "uint8"),
+    "vq": ("sbuf", [128, 128], "float8_e4m3fn_x4"), "vs": ("sbuf", [128, 128], "uint8"),
+    "wq": ("sbuf", [128, 512], "float8_e4m3fn_x4"), "wqs": ("sbuf", [128, 512], "uint8"),
+    "sei": ("sbuf", [128, 20], "int32"),
+    "idt": ("sbuf", [128, 128], "bfloat16"), "eb": ("sbuf", [128, 2048], "bfloat16"),
+    "eq": ("sbuf", [128, 512], "float8_e4m3fn_x4"), "es": ("sbuf", [128, 512], "uint8"),
+    "pi": ("sbuf", [128, 1], "int32"), "li": ("sbuf", [128, 1], "int32"), "lf": ("sbuf", [128, 1], "float32"),
+    "i16": ("sbuf", [128, 320], "float32"), "i512": ("sbuf", [128, 512], "float32"),
+    "ma1": ("sbuf", [128, 320], "bfloat16"), "ma2": ("sbuf", [128, 320], "bfloat16"), "d0r": ("sbuf", [128, 320], "bfloat16"),
+    "la": ("sbuf", [128, 320], "float32"), "lb": ("sbuf", [128, 320], "float32"), "d0l": ("sbuf", [128, 320], "float32"),
+    "subl": ("sbuf", [128, 1], "float32"), "i8": ("sbuf", [128, 80], "float32"), "d0t": ("sbuf", [128, 80], "float32"),
+    "x4": ("sbuf", [128, 4], "int32"), "t4": ("sbuf", [128, 4], "int32"), "w4": ("sbuf", [128, 4], "float32"),
+    "bo": ("sbuf", [128, 4], "float32"), "m4": ("sbuf", [128, 4], "float32"), "oh": ("sbuf", [128, 4], "float32"),
+    "fl0": ("sbuf", [128, 1], "float32"), "ini": ("sbuf", [128, 1], "float32"), "tr": ("sbuf", [128, 1], "float32"),
+    "z8": ("sbuf", [128, 8], "float32"), "ji": ("sbuf", [128, 32], "float32"),
+    "fc": ("sbuf", [128, 128], "float32"), "fm": ("sbuf", [128, 128], "float32"), "fs": ("sbuf", [128, 128], "float32"),
+    "tl": ("sbuf", [128, 8], "uint16"), "tls": ("sbuf", [128, 6], "uint16"),
+    "uli": ("sbuf", [128, 8], "int32"), "ull": ("sbuf", [128, 8], "uint16"),
+    "ai": ("sbuf", [128, 20], "int32"), "si": ("sbuf", [128, 20], "int32"), "ci": ("sbuf", [128, 20], "int32"), "oi": ("sbuf", [128, 20], "int32"),
+    "ofl": ("sbuf", [128, 20], "uint16"), "parl": ("sbuf", [128, 20], "uint16"), "dd": ("sbuf", [128, 656], "float32"),
+    "wo": ("sbuf", [128, 8], "uint16"), "g16": ("sbuf", [128, 64], "float32"), "yt": ("sbuf", [128, 8], "float32"), "yo": ("sbuf", [128, 8], "float32"),
+    "gg": ("sbuf", [128, 512], "float32"), "gs": ("sbuf", [128, 512], "float32"),
+    "ls": ("sbuf", [128, 36], "uint16"), "yf": ("sbuf", [128, 36], "float32"),
+    "lab": ("sbuf", [128, 80], "float32"), "eqv": ("sbuf", [128, 80], "float32"), "eqr": ("sbuf", [128, 8], "float32"),
+    "cs": ("sbuf", [128, 88], "float32"), "c32": ("sbuf", [128, 32], "float32"), "z32": ("sbuf", [128, 32], "float32"),
+    "a32": ("sbuf", [128, 32], "float32"), "n32": ("sbuf", [128, 32], "float32"), "b32": ("sbuf", [128, 32], "float32"),
+    "o32": ("sbuf", [128, 32], "float32"), "ol": ("sbuf", [128, 32], "uint16"), "at": ("sbuf", [128, 960], "float32"),
+    "als": ("sbuf", [128, 320], "float32"), "al": ("sbuf", [128, 20], "uint16"),
+    "tb": ("sbuf", [128, 320], "bfloat16"), "mg": ("sbuf", [128, 320], "bfloat16"), "sc": ("sbuf", [128, 320], "bfloat16"),
+    "e0": ("sbuf", [128, 80], "float32"), "e1": ("sbuf", [128, 80], "float32"), "pp": ("sbuf", [128, 88], "float32"),
+    "prep": ("sbuf", [128, 512], "float32"), "brep": ("sbuf", [128, 320], "float32"), "bsc": ("sbuf", [128, 320], "float32"), "bl": ("sbuf", [128, 20], "uint16"),
+    "zt": ("sbuf", [128, 512], "float32"), "msc": ("sbuf", [128, 320], "float32"), "ml": ("sbuf", [128, 20], "uint16"),
+    "mr": ("sbuf", [128, 320], "float32"), "ysb": ("sbuf", [128, 320], "float32"),
+}
+for _n in ("fw", "fg", "aw"):
+    SCRATCH[_n] = ("sbuf", [128, 1280], "bfloat16")
+for _n in ("pl", "pa", "ll"):
+    SCRATCH[_n] = ("sbuf", [128, 96], "uint16")
+SCRATCH["lr"] = ("sbuf", [128, 1536], "float32")
+for _r in range(4):
+    SCRATCH["q%d" % _r] = ("sbuf", [128, 320], "float8_e4m3fn_x4")
+    SCRATCH["qs%d" % _r] = ("sbuf", [128, 320], "uint8")
+for _r in range(3):
+    SCRATCH["xr%d" % _r] = ("sbuf", [128, 1280], "bfloat16")
+    SCRATCH["hb%d" % _r] = ("sbuf", [128, 1280], "bfloat16")
+    SCRATCH["hq%d" % _r] = ("sbuf", [128, 320], "float8_e4m3fn_x4")
+    SCRATCH["hs%d" % _r] = ("sbuf", [128, 320], "uint8")
+    SCRATCH["lq%d" % _r] = ("sbuf", [128, 320], "float8_e4m3fn_x4")
+    SCRATCH["lqs%d" % _r] = ("sbuf", [128, 320], "uint8")
+
+SEMAPHORES = ["cV", "cS", "cT", "cG", "sent", "stored", "lse", "lx", "lu", "lv", "lwc", "lws"]
+for _r in range(3):
+    SEMAPHORES += ["pr%d" % _r, "lb%d" % _r, "cr%d" % _r, "sr%d" % _r]
+
+
+def rank_program(g, core, T, topo):
+    rank = T.rank_of(core)
+    if rank is None:
+        return
+    eng = {"V": g.vector, "S": g.scalar, "T": g.tensor, "G": g, "Y": g.sync}
+    cnt = {"V": 0, "S": 0, "T": 0, "G": 0}
+    known = {q: {} for q in eng}
+    lastw, readers = {}, {}
+
+    def wait(q, stamp):
+        sem, val = stamp
+        if known[q].get(sem, 0) < val:
+            eng[q].wait_ge(T.sem[sem], val)
+            known[q][sem] = val
+
+    def order(q, r, w):
+        need = {}
+        for t in r:
+            if t in lastw: need[lastw[t][0]] = max(need.get(lastw[t][0], 0), lastw[t][1])
+        for t in w:
+            if t in lastw: need[lastw[t][0]] = max(need.get(lastw[t][0], 0), lastw[t][1])
+            for s, v in readers.get(t, []): need[s] = max(need.get(s, 0), v)
+        for s in sorted(need): wait(q, (s, need[s]))
+
+    def mark(r, w, stamp):
+        for t in r: readers.setdefault(t, []).append(stamp)
+        for t in w:
+            lastw[t] = stamp
+            readers[t] = []
+
+    def op(q, call, r, w):
+        bank = [t for t in r if t.startswith("bank")]
+        r, w = [t for t in r if t not in bank], list(w) + bank
+        order(q, r, w)
+        cnt[q] += 1
+        call(eng[q]).then_inc(T.sem["c" + q], 1)
+        mark(r, w, ("c" + q, cnt[q]))
+
+    def load(q, out, in_, w, sem):
+        eng[q].dma_start(out, in_).then_inc(T.sem[sem], 16)
+        mark([], [w], (sem, 16))
+
+    stores = [0]
+
+    def store(q, out, in_, r):
+        order(q, r, [])
+        eng[q].dma_start(out, in_).then_inc(T.sem.stored, 16)
+        stores[0] += 16
+
+    def vts(out, in0, s1, s2, op0, op1, r, w):
+        if op1 is None: op("V", lambda e: e.tensor_scalar(out, in0, s1, s2, op0), r, w)
+        else: op("V", lambda e: e.tensor_scalar(out, in0, s1, s2, op0, op1), r, w)
+
+    def vtt(out, a, b, o, r, w): op("V", lambda e: e.tensor_tensor(out, a, b, o), r, w)
+    def vcp(out, in_, r, w): op("V", lambda e: e.tensor_copy(out, in_), r, w)
+    def vset(ap, c, w): op("V", lambda e: e.memset(ap, c), [], w)
+    def vscan(out, d0, d1, ini, o0, o1, r, w): op("V", lambda e: e.tensor_tensor_scan(out, d0, d1, ini, o0, o1), r, w)
+    def iota(ap, pat, base, cm, w): op("G", lambda e: e.iota(ap, pat, base, cm, allow_small_or_imprecise_dtypes=True), [], w)
+    def act(out, in_, r, w, **k): op("S", lambda e: e.activation(out, in_, COPY, **k), r, w)
+    def quant(c, s, t, r, w): op("V", lambda e: e.quantize_mx(c, s, t), r, w)
+
+    def mm(bank, lc, lsc, rc, rsc, r):
+        out = T.ps[:, 512 * bank:512 * bank + C]
+        op("T", lambda e: e.matmul_mx(out, lc, lsc, rc, rsc, True, True), r, ["bank%d" % bank])
+
+    def bank(b): return T.ps[:, 512 * b:512 * b + C]
+
+    sent = [0]
+
+    def send(out, in_, rsem, dst, r):
+        order("G", r, [])
+        rid, pid, _s = topo.addr(dst)
+        g.remote_dma(out, in_, T.sem[rsem], T.sem.sent, pid, rid, topo.mask(core, dst))
+        sent[0] += len(topo.engines(core, dst))
+
+    partner = [T.cores[rank ^ s] for s in STEP]
+
+    load("Y", T.sei[:, :], T.se[:, :], "sei", "lse")
+    load("S", T.ub[:, :], T.u[:, :], "ub", "lu")
+    load("Y", T.x0[:, :], T.x[:, :], "x0", "lx")
+    load("S", T.wq[:, :].bitcast(dt.uint8), T.wc[:, :], "wq", "lwc")
+    load("Y", T.wqs[:, :], T.ws[:, :], "wqs", "lws")
+    load("S", T.vb[:, :], T.v[:, :], "vb", "lv")
+
+    op("G", lambda e: e.iota(T.pi[:, :], [[0, 1]], 0, 1), [], ["pi"])
+    iota(T.i16[:, :], [[0, 20], [1, 16]], 0, 0, ["i16"])
+    iota(T.i512[:, :], [[1, 512]], 0, 0, ["i512"])
+    op("G", lambda e: e.iota(T.uli[:, :], [[16, 8]], 0, 0), [], ["uli"])
+    vset(T.idt[:, :], 0.5, ["idt"])
+    vset(T.eb[:, :], 0.0, ["eb"])
+    vset(T.fc[:, :], 15.0, ["fc"])
+    vset(T.e0[:, :], 0.0, ["e0"])
+    vset(T.z8[:, :], 0.0, ["z8"])
+    vset(T.yt[:, :], 0.0, ["yt0"])
+    vset(T.ls[:, :], 0, ["ls31", "lst", "ls8", "ls7", "ls6", "ls5", "ls4"])
+    vts(T.li[:, :], T.pi[:, :], 15, None, A.bitwise_and, None, ["pi"], ["li"])
+    vcp(T.lf[:, :], T.li[:, :], ["li"], ["lf"])
+    for j in range(4):
+        vts(T.x4[:, j:j + 1], T.li[:, :], 8 >> j, None, A.bitwise_and, None, ["li"], ["x4%d" % j])
+    for j in range(4):
+        vts(T.bo[:, j:j + 1], T.x4[:, j:j + 1], float(40 << j), None, A.mult, None, ["x4%d" % j], ["bo%d" % j])
+    vcp(T.wo[:, 0:1], T.bo[:, 0:1], ["bo0"], ["wo0"])
+    vts(T.ma1[:, :], T.i16[:, :], T.lf[:, 0:1], None, A.is_equal, None, ["i16", "lf"], ["ma1"])
+    vts(T.d0r[:, :], T.i16[:, :], 0.0, None, A.not_equal, None, ["i16"], ["d0r"])
+    vts(T.tr[:, :], T.lf[:, :], 0.0, 640.0, A.is_equal, A.mult, ["lf"], ["tr"])
+    act(T.dd[:, 0:C], T.i512[:, 0:C], ["i512"], ["dd"])
+    act(T.dd[:, C:2 * C], T.i512[:, 0:C], ["i512"], ["dd1"])
+    op("G", lambda e: e.affine_select(T.idt[:, :], T.idt[:, :], [[-1, 128]], A.is_equal, 0.0, 0, 1), ["idt"], ["idt"])
+    for j in range(4):
+        iota(T.fc[:, j:80:8], [[0, 10]], 271 + 16 * j, 0, ["fc"])
+    iota(T.fc[:, 20:80:8], [[0, 8]], 239, 0, ["fc"])
+    iota(T.fc[:, 21:80:8], [[0, 4], [16, 2]], 207, 0, ["fc"])
+    iota(T.fc[:, 22:80:8], [[0, 2], [16, 4]], 143, 0, ["fc"])
+    iota(T.fc[:, 23:80:8], [[16, 8]], 15, 0, ["fc"])
+    iota(T.fc[:, 96:104], [[8, 8]], 23, 0, ["fc"])
+    iota(T.fc[:, 104:112], [[1, 8]], 80, 0, ["fc"])
+    iota(T.fc[:, 112:120], [[8, 8]], 22, 0, ["fc"])
+    iota(T.fc[:, 120:124], [[8, 4]], 21, 0, ["fc"])
+    iota(T.fc[:, 124:126], [[8, 2]], 20, 0, ["fc"])
+    iota(T.fc[:, 126:128], [[-12, 2]], 19, 0, ["fc"])
+    iota(T.e0[:, 20:80:8], [[0, 4], [16, 2]], -8, 0, ["e0"])
+    iota(T.e0[:, 21:80:8], [[0, 2], [8, 2], [0, 2]], -4, 0, ["e0"])
+    iota(T.e0[:, 22:80:8], [[4, 2], [0, 4]], -2, 0, ["e0"])
+    iota(T.e0[:, 23:80:8], [[0, 8]], -1, 0, ["e0"])
+    iota(T.i8[:, :], [[0, 10], [1, 8]], 0, 0, ["i8"])
+    iota(T.ji[:, :], [[16, 32]], 320, 1, ["ji"])
+
+    vts(T.si[:, :], T.sei[:, :], 1, None, A.bitwise_and, None, ["sei"], ["si"])
+    vts(T.ai[:, :], T.sei[:, :], 1, None, A.arith_shift_right, None, ["sei"], ["ai"])
+    vts(T.ci[:, :], T.si[:, :], 320.0, None, A.mult, None, ["si"], ["ci"])
+    vtt(T.oi[:, :], T.ci[:, :], T.ai[:, :], A.add, ["ci", "ai"], ["oi"])
+    vcp(T.ofl[:, 1:20], T.oi[:, 1:20], ["oi"], ["ofl"])
+    vts(T.ofl[:, 0:1], T.oi[:, 0:1], T.tr[:, 0:1], None, A.add, None, ["oi", "tr"], ["ofl0"])
+    vcp(T.dd[:, 0:656].indirect(T.ofl[:, 0:20]), T.i512[:, 0:C], ["ofl", "ofl0", "i512"], ["dd", "dd1"])
+    vcp(T.ull[:, :], T.uli[:, :], ["uli"], ["ull"])
+    vcp(T.parl[:, :], T.ai[:, :], ["ai"], ["parl"])
+    for j in range(4):
+        vtt(T.g16[:, 16 * j:16 * j + 16], T.dd[:, 0:2 * C].indirect(T.wo[:, 2 * j:2 * j + 1]), T.ma1[:, 0:16], A.mult,
+            ["dd", "dd1", "wo%d" % j, "ma1"], ["g16%d" % j])
+        op("V", lambda e: e.tensor_reduce(T.yt[:, j + 1:j + 2], T.g16[:, 16 * j:16 * j + 16], AxisListType.X, A.add), ["g16%d" % j], ["yt%d" % (j + 1)])
+        if j < 3:
+            vts(T.wo[:, 2 * j + 2:2 * j + 3], T.yt[:, j + 1:j + 2], T.bo[:, j + 1:j + 2], None, A.add, None, ["yt%d" % (j + 1), "bo%d" % (j + 1)], ["wo%d" % (j + 1)])
+        else:
+            vcp(T.ls[:, 30:31], T.yt[:, 4:5], ["yt4"], ["ls4"])
+    vcp(T.ls[:, 32:36], T.yt[:, 0:4], ["yt0", "yt1", "yt2", "yt3"], ["lst"])
+
+    quant(T.q0[:, 0:C], T.qs0[:, 0:C], T.x0[:, 0:1280], ["x0"], ["q0"])
+    quant(T.uq[:, :], T.us[:, :], T.ub[:, :], ["ub"], ["uq"])
+    vcp(T.ur[:, 0:128].bitcast(dt.uint32), T.uq[:, 0:128].bitcast(dt.uint32).indirect(T.ull[:, 0:8]), ["uq", "ull"], ["ur"])
+    act(T.urs[:, 0:128], T.us[:, 0:128].indirect(T.ull[:, 0:8]), ["uq", "ull"], ["urs"])
+
+    for n, s0, s1, a, b in ((1, 30, 28, "ls4", "ls5"), (2, 28, 24, "ls5", "ls6"), (4, 24, 16, "ls6", "ls7"), (8, 16, 0, "ls7", "ls8")):
+        k = 16 * n
+        if n == 8:
+            vts(T.ma2[:, :], T.ma1[:, :], 2.0, None, A.mult, None, ["ma1"], ["ma2"])
+        vtt(T.gg[:, 0:k], T.dd[:, 0:C].indirect(T.ls[:, s0:s0 + n]), T.ma1[:, 0:k], A.mult, ["dd", a, "ma1"], ["gga"])
+        vtt(T.gg[:, k:2 * k], T.dd[:, C:2 * C].indirect(T.ls[:, s0:s0 + n]), T.ma1[:, 0:k], A.mult, ["dd1", a, "ma1"], ["ggb"])
+        vscan(T.gs[:, 0:2 * k], T.d0r[:, 0:2 * k], T.gg[:, 0:2 * k], 0.0, A.mult, A.add, ["gga", "ggb", "d0r"], ["gs"])
+        vcp(T.ls[:, s1:s1 + 2 * n], T.gs[:, 15:2 * k:16], ["gs"], [b])
+    for j in range(3):
+        vts(T.t4[:, j:j + 1], T.li[:, :], 7 >> j, None, A.bitwise_and, None, ["li"], ["t4"])
+    vset(T.t4[:, 3:4], 0, ["t4"])
+    vts(T.m4[:, :], T.t4[:, :], 0.0, None, A.not_equal, None, ["t4"], ["m4"])
+    vtt(T.oh[:, 0:3], T.m4[:, 0:3], T.m4[:, 1:4], A.subtract, ["m4"], ["oh"])
+    vtt(T.yo[:, 0:3], T.yt[:, 1:4], T.oh[:, 0:3], A.mult, ["oh", "yt1", "yt2", "yt3"], ["yo"])
+    op("V", lambda e: e.tensor_reduce(T.yo[:, 4:5], T.yo[:, 0:3], AxisListType.X, A.add), ["yo"], ["yo4"])
+    vcp(T.ls[:, 31:32], T.yo[:, 4:5], ["yo4"], ["ls31"])
+    LS = ["ls31", "lst", "ls8", "ls7", "ls6", "ls5", "ls4"]
+
+    def labels(k):
+        send(T.ll[:, 32 * k:32 * k + 32], T.ls[:, 0:32], "lb%d" % k, partner[k], LS)
+
+    labels(0)
+
+    for j in range(4):
+        vts(T.w4[:, j:j + 1], T.x4[:, j:j + 1], 32.0, float(-(128 >> j)), A.mult, A.add, ["x4%d" % j], ["w4"])
+    for j in range(4):
+        vts(T.e0[:, 16 + j:80:8], T.z8[:, :], T.w4[:, j:j + 1], None, A.add, None, ["z8", "w4"], ["e0"])
+    vtt(T.e0[:, 0:4], T.w4[:, :], T.m4[:, :], A.mult, ["w4", "m4"], ["e0"])
+    vts(T.fl0[:, :], T.lf[:, :], 0.0, None, A.is_equal, None, ["lf"], ["fl0"])
+    vts(T.ini[:, :], T.fl0[:, :], -256.0, None, A.mult, None, ["fl0"], ["ini"])
+    vts(T.d0t[:, :], T.i8[:, :], 0.0, None, A.not_equal, None, ["i8"], ["d0t"])
+    vset(T.d0t[:, 0:1], 1.0, ["d0t"])
+    vtt(T.fm[:, :], T.fc[:, :], T.ma1[:, 0:128], A.mult, ["fc", "ma1"], ["fm"])
+    vscan(T.fs[:, :], T.d0r[:, 0:128], T.fm[:, :], 0.0, A.mult, A.add, ["fm", "d0r"], ["fs"])
+    vcp(T.tl[:, 0:8], T.fs[:, 15:128:16], ["fs"], ["tl"])
+
+    ee = ["e0", "e1"]
+    for r in range(3):
+        q, qs, qt = T["q%d" % r], T["qs%d" % r], "q%d" % r
+        Q, QS = q[:, 0:C], qs[:, 0:C]
+        mm(0, T.ur[:, 0:128], T.urs[:, 0:128], Q, QS, [qt, "ur", "urs"])
+        for b in range(4):
+            mm(1 + b, T.wq[:, 128 * b:128 * b + 128], T.wqs[:, 128 * b:128 * b + 128], Q, QS, [qt, "wq", "wqs"])
+        vts(T.tb[:, :], bank(0), 0.0, 0.5, A.is_ge, A.subtract, ["bank0"], ["tb"])
+        vtt(T.mg[:, :], T.tb[:, 0:C].indirect(T.ls[:, 16:36]), T.ma2[:, :], A.mult, ["tb", "ma2"] + LS, ["mg"])
+        vscan(T.sc[:, :], T.d0r[:, :], T.mg[:, :], 0.0, A.mult, A.add, ["mg", "d0r"], ["sc"])
+        eo, en = ee[r % 2], ee[(r + 1) % 2]
+        vtt(T[en][:, :], T.sc[:, 0:C].indirect(T.tl[:, 0:5]), T[eo][:, :], A.mult, ["sc", "tl", eo], [en])
+        vscan(T.pp[:, 0:80], T.d0t[:, :], T[en][:, :], T.ini[:, 0:1], A.mult, A.add, [en, "d0t", "ini"], ["pp"])
+        vtt(T.pp[:, 80:88], T.pp[:, 22:80:8], T[en][:, 23:80:8], A.subtract, ["pp", en], ["ppr"])
+        pl, pa = T.pl[:, 32 * r:32 * r + 32], T.pa[:, 32 * r:32 * r + 32]
+        vts(pl, T.pp[:, 0:88].indirect(T.tl[:, 6:8]), 256.0, None, A.add, None, ["pp", "ppr", "tl"], ["pl%d" % r])
+        send(pa, pl, "pr%d" % r, partner[r], ["pl%d" % r])
+        hb = T["hb%d" % r]
+        for b in range(4):
+            act(hb[:, b:1280:4], bank(1 + b), ["bank%d" % (1 + b)], ["hb%d.%d" % (r, b)], scale=0.03125)
+        quant(T["hq%d" % r][:, 0:C], T["hs%d" % r][:, 0:C], hb[:, 0:1280], ["hb%d.%d" % (r, b) for b in range(4)], ["hq%d" % r])
+        send(T["lq%d" % r][:, 0:C].bitcast(dt.uint8), T["hq%d" % r][:, 0:C].bitcast(dt.uint8), "cr%d" % r, partner[r], ["hq%d" % r])
+        send(T["lqs%d" % r][:, 0:C], T["hs%d" % r][:, 0:C], "sr%d" % r, partner[r], ["hq%d" % r])
+        if r == 0:
+            labels(1)
+            labels(2)
+            for b in range(4):
+                vcp(T.eb[:, 512 * b + b:512 * b + 512:4], T.idt[:, :], ["idt", "eb"], ["eb%d" % b])
+            quant(T.eq[:, :], T.es[:, :], T.eb[:, :], ["eb0", "eb1", "eb2", "eb3"], ["eq"])
+        fb = [5, 6, 7, 0]
+        for b in range(4):
+            mm(fb[b], T.eq[:, 128 * b:128 * b + 128], T.es[:, 128 * b:128 * b + 128], Q, QS, [qt, "eq"])
+        if r == 0:
+            vts(T.la[:, :], T.i16[:, :], T.lf[:, 0:1], None, A.subtract, None, ["i16", "lf"], ["la"])
+            vts(T.lb[:, :], T.la[:, :], 0.0, -65536.0, A.is_equal, A.mult, ["la"], ["lb"])
+            vts(T.la[:, :], T.la[:, :], 1.0, 1024.0, A.is_equal, A.mult, ["la", "lb"], ["la"])
+            vtt(T.d0l[:, :], T.la[:, :], T.lb[:, :], A.add, ["la", "lb"], ["d0l"])
+            vts(T.subl[:, :], T.lf[:, :], 15.0, 1024.0, A.not_equal, A.mult, ["lf"], ["subl"])
+            vts(T.tls[:, 0:5], T.fs[:, 15:80:16], 0.0625, 15.0625, A.mult, A.add, ["fs"], ["tls"])
+            vcp(T.yf[:, :], T.ls[:, :], LS, ["yf"])
+            vcp(T.lab[:, :], T.yf[:, 0:36].indirect(T.tls[:, 0:5]), ["yf", "tls"], ["lab"])
+            vset(T.eqv[:, :], 0.0, ["eqv"])
+            vtt(T.eqv[:, 0:79], T.lab[:, 1:80], T.lab[:, 0:79], A.is_equal, ["lab"], ["eqv"])
+            vtt(T.eqv[:, 23:80:8], T.lab[:, 23:80:8], T.yf[:, 0:8], A.is_equal, ["lab", "yf"], ["eqv"])
+            vtt(T.eqr[:, :], T.lab[:, 23:80:8], T.yf[:, 8:16], A.is_equal, ["lab", "yf"], ["eqr"])
+            vtt(T.eqv[:, 0:4], T.eqv[:, 0:4], T.m4[:, :], A.mult, ["eqv", "m4"], ["eqv"])
+            vset(T.eqv[:, 4:8], 0.0, ["eqv"])
+            vscan(T.cs[:, 0:80], T.d0t[:, :], T.eqv[:, :], T.fl0[:, 0:1], A.mult, A.add, ["eqv", "d0t", "fl0"], ["cs"])
+            vtt(T.cs[:, 80:88], T.cs[:, 22:80:8], T.eqr[:, :], A.add, ["cs", "eqr"], ["csr"])
+            vcp(T.c32[:, :], T.cs[:, 0:88].indirect(T.tl[:, 6:8]), ["cs", "csr", "tl"], ["c32"])
+            vts(T.z32[:, :], T.c32[:, :], 0.0, None, A.is_equal, None, ["c32"], ["z32"])
+            vts(T.n32[:, :], T.c32[:, :], 0.0, None, A.is_gt, None, ["c32"], ["n32"])
+            vtt(T.a32[:, :], T.z32[:, :], T.yf[:, 0:32], A.mult, ["z32", "yf"], ["a32"])
+            vtt(T.b32[:, :], T.n32[:, :], T.ji[:, :], A.mult, ["n32", "ji"], ["b32"])
+            vtt(T.o32[:, :], T.a32[:, :], T.b32[:, :], A.add, ["a32", "b32"], ["o32"])
+            vcp(T.ol[:, :], T.o32[:, :], ["o32"], ["ol"])
+            vcp(T.at[:, 0:960].indirect(T.ol[:, 0:32]), T.i512[:, :], ["ol", "i512"], ["at"])
+            vscan(T.als[:, :], T.d0l[:, :], T.at[:, 0:C], 0.0, A.add, A.max, ["at", "d0l"], ["als"])
+            vts(T.al[:, :], T.als[:, 15:C:16], T.subl[:, 0:1], None, A.subtract, None, ["als", "subl"], ["al"])
+        act(T.prep[:, :], T.i512[:, :].indirect(pl), ["i512", "pl%d" % r], ["prep"])
+        act(T.brep[:, :], T.prep[:, :].indirect(T.al[:, 0:20]), ["prep", "al"], ["brep"])
+        for b in range(4):
+            vcp(T.fw[:, C * b:C * b + C], bank(fb[b]), ["bank%d" % fb[b]], ["fw%d" % b])
+        vscan(T.bsc[:, :], T.d0l[:, :], T.brep[:, :], 0.0, A.add, A.max, ["brep", "d0l"], ["bsc"])
+        vts(T.bl[:, :], T.bsc[:, 15:C:16], T.subl[:, 0:1], None, A.subtract, None, ["bsc", "subl"], ["bl"])
+        if r == 0:
+            lastw["ll0"] = ("lb0", len(topo.engines(core, partner[0])))
+            act(T.lr[:, 0:512], T.i512[:, 0:C].indirect(T.ll[:, 0:32]), ["i512", "ll0"], ["lr0"])
+        for b in range(4):
+            act(T.fg[:, C * b:C * b + C], T.fw[:, C * b:C * b + C].indirect(T.parl[:, 0:20]), ["fw%d" % b, "parl"], ["fg%d" % b])
+        k = len(topo.engines(core, partner[r]))
+        lastw["pa%d" % r], lastw["lq%d" % r], lastw["lqs%d" % r] = ("pr%d" % r, k), ("cr%d" % r, k), ("sr%d" % r, k)
+        vcp(T.zt[:, :].indirect(pa), T.lr[:, 512 * r:512 * r + 512], ["pa%d" % r, "lr%d" % r], ["zt"])
+        vcp(T.mr[:, :], T.zt[:, :].indirect(T.bl[:, 0:20]), ["zt", "bl"], ["mr"])
+        vscan(T.msc[:, :], T.d0l[:, :], T.mr[:, :], 0.0, A.add, A.max, ["mr", "d0l"], ["msc"])
+        vts(T.ml[:, :], T.msc[:, 15:C:16], T.subl[:, 0:1], None, A.subtract, None, ["msc", "subl"], ["ml"])
+        if r == 2:
+            store("Y", T.im[:, :], T.mr[0:128:16, :], ["mr"])
+        for b in range(4):
+            mm(1 + b, T.eq[:, 128 * b:128 * b + 128], T.es[:, 128 * b:128 * b + 128], T["lq%d" % r][:, 0:C], T["lqs%d" % r][:, 0:C], ["lq%d" % r, "lqs%d" % r, "eq"])
+        for b in range(4):
+            act(T.aw[:, C * b:C * b + C], bank(1 + b), ["bank%d" % (1 + b)], ["aw%d" % b])
+        xr = T["xr%d" % r]
+        for b in range(4):
+            vtt(xr[:, b:1280:4], T.aw[:, C * b:C * b + C].indirect(T.ml[:, 0:20]), T.fg[:, C * b:C * b + C], A.add, ["aw%d" % b, "ml", "fg%d" % b], ["xr%d.%d" % (r, b)])
+        n = r + 1
+        quant(T["q%d" % n][:, 0:C], T["qs%d" % n][:, 0:C], xr[:, 0:1280], ["xr%d.%d" % (r, b) for b in range(4)], ["q%d" % n])
+        if r < 2:
+            lastw["ll%d" % n] = ("lb%d" % n, len(topo.engines(core, partner[n])))
+            act(T.lr[:, 512 * n:512 * n + 512], T.i512[:, 0:C].indirect(T.ll[:, 32 * n:32 * n + 32]), ["i512", "ll%d" % n], ["lr%d" % n])
+        if r == 0:
+            quant(T.vq[:, :], T.vs[:, :], T.vb[:, :], ["vb"], ["vq"])
+
+    mm(5, T.vq[:, 0:128], T.vs[:, 0:128], T.q3[:, 0:C], T.qs3[:, 0:C], ["q3", "vq"])
+    store("Y", T.oc[:, :], T.q3[:, 0:C].bitcast(dt.uint8), ["q3"])
+    for k in range(4):
+        store("S" if k % 2 else "Y", T.osc[4 * k:4 * k + 4, :], T.qs3[32 * k:32 * k + 4, 0:C], ["q3"])
+    vcp(T.ysb[:, :], bank(5), ["bank5"], ["ysb"])
+    store("Y", T.y[:, :], T.ysb[:, :], ["ysb"])
+    for k in ("V", "S", "T", "G"):
+        wait("G", ("c" + k, cnt[k]))
+    g.wait_ge(T.sem.stored, stores[0])
+    g.wait_ge(T.sem.sent, sent[0])

@@ -4,51 +4,31 @@ from concourse.mybir import dt, AluOpType, AxisListType, ActivationFunctionType
 C = 320
 STEP = [1, 2, 4]
 A = AluOpType
-COPY = ActivationFunctionType.Copy
+F = ActivationFunctionType
 
-SCRATCH = {
-    "ps": ("psum", [128, 4096], "float32"),
-    "x0": ("sbuf", [128, 1280], "bfloat16"), "ub": ("sbuf", [128, 512], "bfloat16"), "vb": ("sbuf", [128, 512], "bfloat16"),
-    "uq": ("sbuf", [128, 128], "float8_e4m3fn_x4"), "us": ("sbuf", [128, 128], "uint8"),
-    "ur": ("sbuf", [128, 128], "float8_e4m3fn_x4"), "urs": ("sbuf", [128, 128], "uint8"),
-    "vq": ("sbuf", [128, 128], "float8_e4m3fn_x4"), "vs": ("sbuf", [128, 128], "uint8"),
-    "wq": ("sbuf", [128, 512], "float8_e4m3fn_x4"), "wqs": ("sbuf", [128, 512], "uint8"),
-    "sei": ("sbuf", [128, 20], "int32"),
-    "idt": ("sbuf", [128, 128], "bfloat16"), "eb": ("sbuf", [128, 2048], "bfloat16"),
-    "eq": ("sbuf", [128, 512], "float8_e4m3fn_x4"), "es": ("sbuf", [128, 512], "uint8"),
-    "pi": ("sbuf", [128, 1], "int32"), "li": ("sbuf", [128, 1], "int32"), "lf": ("sbuf", [128, 1], "float32"),
-    "i16": ("sbuf", [128, 320], "float32"), "i512": ("sbuf", [128, 512], "float32"),
-    "ma1": ("sbuf", [128, 320], "bfloat16"), "ma2": ("sbuf", [128, 320], "bfloat16"), "d0r": ("sbuf", [128, 320], "bfloat16"),
-    "la": ("sbuf", [128, 320], "float32"), "lb": ("sbuf", [128, 320], "float32"), "d0l": ("sbuf", [128, 320], "float32"),
-    "subl": ("sbuf", [128, 1], "float32"), "i8": ("sbuf", [128, 80], "float32"), "d0t": ("sbuf", [128, 80], "float32"),
-    "x4": ("sbuf", [128, 4], "int32"), "t4": ("sbuf", [128, 4], "int32"), "w4": ("sbuf", [128, 4], "float32"),
-    "bo": ("sbuf", [128, 4], "float32"), "m4": ("sbuf", [128, 4], "float32"), "oh": ("sbuf", [128, 4], "float32"),
-    "fl0": ("sbuf", [128, 1], "float32"), "ini": ("sbuf", [128, 1], "float32"), "tr": ("sbuf", [128, 1], "float32"),
-    "z8": ("sbuf", [128, 8], "float32"), "ji": ("sbuf", [128, 32], "float32"),
-    "fc": ("sbuf", [128, 128], "float32"), "fm": ("sbuf", [128, 128], "float32"), "fs": ("sbuf", [128, 128], "float32"),
-    "tl": ("sbuf", [128, 8], "uint16"), "tls": ("sbuf", [128, 6], "uint16"),
-    "uli": ("sbuf", [128, 8], "int32"), "ull": ("sbuf", [128, 8], "uint16"),
-    "ai": ("sbuf", [128, 20], "int32"), "si": ("sbuf", [128, 20], "int32"), "ci": ("sbuf", [128, 20], "int32"), "oi": ("sbuf", [128, 20], "int32"),
-    "ofl": ("sbuf", [128, 20], "uint16"), "parl": ("sbuf", [128, 20], "uint16"), "dd": ("sbuf", [128, 656], "float32"),
-    "wo": ("sbuf", [128, 8], "uint16"), "g16": ("sbuf", [128, 64], "float32"), "yt": ("sbuf", [128, 8], "float32"), "yo": ("sbuf", [128, 8], "float32"),
-    "gg": ("sbuf", [128, 512], "float32"), "gs": ("sbuf", [128, 512], "float32"),
-    "ls": ("sbuf", [128, 36], "uint16"), "yf": ("sbuf", [128, 36], "float32"),
-    "lab": ("sbuf", [128, 80], "float32"), "eqv": ("sbuf", [128, 80], "float32"), "eqr": ("sbuf", [128, 8], "float32"),
-    "cs": ("sbuf", [128, 88], "float32"), "c32": ("sbuf", [128, 32], "float32"), "z32": ("sbuf", [128, 32], "float32"),
-    "a32": ("sbuf", [128, 32], "float32"), "n32": ("sbuf", [128, 32], "float32"), "b32": ("sbuf", [128, 32], "float32"),
-    "o32": ("sbuf", [128, 32], "float32"), "ol": ("sbuf", [128, 32], "uint16"), "at": ("sbuf", [128, 960], "float32"),
-    "als": ("sbuf", [128, 320], "float32"), "al": ("sbuf", [128, 20], "uint16"),
-    "tb": ("sbuf", [128, 320], "bfloat16"), "mg": ("sbuf", [128, 320], "bfloat16"), "sc": ("sbuf", [128, 320], "bfloat16"),
-    "e0": ("sbuf", [128, 80], "float32"), "e1": ("sbuf", [128, 80], "float32"), "pp": ("sbuf", [128, 88], "float32"),
-    "prep": ("sbuf", [128, 512], "float32"), "brep": ("sbuf", [128, 320], "float32"), "bsc": ("sbuf", [128, 320], "float32"), "bl": ("sbuf", [128, 20], "uint16"),
-    "zt": ("sbuf", [128, 512], "float32"), "msc": ("sbuf", [128, 320], "float32"), "ml": ("sbuf", [128, 20], "uint16"),
-    "mr": ("sbuf", [128, 320], "float32"), "ysb": ("sbuf", [128, 320], "float32"),
-}
-for _n in ("fw", "fg", "aw"):
-    SCRATCH[_n] = ("sbuf", [128, 1280], "bfloat16")
-for _n in ("pl", "pa", "ll"):
-    SCRATCH[_n] = ("sbuf", [128, 96], "uint16")
-SCRATCH["lr"] = ("sbuf", [128, 1536], "float32")
+SCRATCH = {"ps": ("psum", [128, 4096], "float32")}
+for _n, _w, _d in (
+        ("x0", 1280, "bfloat16"), ("ub", 512, "bfloat16"), ("vb", 512, "bfloat16"), ("sei", 20, "int32"),
+        ("uq", 128, "float8_e4m3fn_x4"), ("us", 128, "uint8"), ("ur", 128, "float8_e4m3fn_x4"), ("urs", 128, "uint8"),
+        ("vq", 128, "float8_e4m3fn_x4"), ("vs", 128, "uint8"), ("wq", 512, "float8_e4m3fn_x4"), ("wqs", 512, "uint8"),
+        ("idt", 128, "bfloat16"), ("eb", 2048, "bfloat16"), ("eq", 512, "float8_e4m3fn_x4"), ("es", 512, "uint8"),
+        ("pi", 1, "int32"), ("li", 1, "int32"), ("lf", 1, "float32"), ("i16", 320, "float32"), ("i512", 512, "float32"),
+        ("ma1", 320, "bfloat16"), ("ma2", 320, "bfloat16"), ("d0r", 320, "bfloat16"), ("d0l", 320, "float32"),
+        ("subl", 1, "float32"), ("i8", 80, "float32"), ("d0t", 80, "float32"), ("x4", 4, "int32"), ("t4", 8, "int32"),
+        ("w4", 4, "float32"), ("bo", 4, "float32"), ("m8", 8, "float32"), ("oh", 4, "float32"), ("fl0", 1, "float32"),
+        ("ini", 1, "float32"), ("tr", 1, "float32"), ("z8", 8, "float32"), ("ji", 32, "float32"), ("fc", 128, "float32"),
+        ("fm", 128, "float32"), ("fs", 128, "float32"), ("tl", 8, "uint16"), ("tls", 6, "uint16"), ("uli", 8, "int32"), ("ull", 8, "uint16"),
+        ("ai", 20, "int32"), ("ofl", 20, "uint16"), ("parl", 20, "uint16"), ("dd", 656, "float32"), ("wo", 8, "uint16"), ("wv", 32, "uint16"),
+        ("g16", 64, "float32"), ("yt", 8, "float32"), ("yo", 8, "float32"), ("gg", 512, "float32"), ("gs", 512, "float32"),
+        ("ls", 36, "uint16"), ("yf", 36, "float32"), ("lab", 80, "float32"), ("eqv", 80, "float32"), ("eqr", 8, "float32"),
+        ("cs", 88, "float32"), ("z32", 32, "float32"), ("y32", 32, "float32"), ("zy", 32, "float32"), ("o32", 32, "float32"), ("ol", 32, "uint16"),
+        ("at", 960, "float32"), ("als", 320, "float32"), ("al", 20, "uint16"),
+        ("tb", 320, "bfloat16"), ("mg", 320, "bfloat16"), ("sc", 320, "bfloat16"), ("e0", 80, "float32"), ("e1", 80, "float32"),
+        ("pp", 88, "float32"), ("prep", 512, "float32"), ("brep", 320, "float32"), ("bsc", 320, "float32"), ("bl", 20, "uint16"),
+        ("zt", 512, "float32"), ("msc", 320, "float32"), ("ml", 20, "uint16"), ("mr", 320, "float32"), ("ysb", 320, "float32"),
+        ("fw", 1280, "bfloat16"), ("fg", 1280, "bfloat16"), ("aw", 1280, "bfloat16"),
+        ("pl", 96, "uint16"), ("pa", 96, "uint16"), ("ll", 96, "uint16"), ("lr", 1536, "float32")):
+    SCRATCH[_n] = ("sbuf", [128, _w], _d)
 for _r in range(4):
     SCRATCH["q%d" % _r] = ("sbuf", [128, 320], "float8_e4m3fn_x4")
     SCRATCH["qs%d" % _r] = ("sbuf", [128, 320], "uint8")
@@ -121,9 +101,10 @@ def rank_program(g, core, T, topo):
     def vtt(out, a, b, o, r, w): op("V", lambda e: e.tensor_tensor(out, a, b, o), r, w)
     def vcp(out, in_, r, w): op("V", lambda e: e.tensor_copy(out, in_), r, w)
     def vset(ap, c, w): op("V", lambda e: e.memset(ap, c), [], w)
+    def vred(out, in_, r, w): op("V", lambda e: e.tensor_reduce(out, in_, AxisListType.X, A.add), r, w)
     def vscan(out, d0, d1, ini, o0, o1, r, w): op("V", lambda e: e.tensor_tensor_scan(out, d0, d1, ini, o0, o1), r, w)
     def iota(ap, pat, base, cm, w): op("G", lambda e: e.iota(ap, pat, base, cm, allow_small_or_imprecise_dtypes=True), [], w)
-    def act(out, in_, r, w, **k): op("S", lambda e: e.activation(out, in_, COPY, **k), r, w)
+    def act(out, in_, r, w, f=F.Copy, **k): op("S", lambda e: e.activation(out, in_, f, **k), r, w)
     def quant(c, s, t, r, w): op("V", lambda e: e.quantize_mx(c, s, t), r, w)
 
     def mm(bank, lc, lsc, rc, rsc, r):
@@ -140,6 +121,14 @@ def rank_program(g, core, T, topo):
         g.remote_dma(out, in_, T.sem[rsem], T.sem.sent, pid, rid, topo.mask(core, dst))
         sent[0] += len(topo.engines(core, dst))
 
+    spare = []
+
+    def later(f, *a): spare.append(lambda: f(*a))
+
+    def fill(n=1):
+        for _i in range(n):
+            if spare: spare.pop(0)()
+
     partner = [T.cores[rank ^ s] for s in STEP]
 
     load("Y", T.sei[:, :], T.se[:, :], "sei", "lse")
@@ -149,110 +138,142 @@ def rank_program(g, core, T, topo):
     load("Y", T.wqs[:, :], T.ws[:, :], "wqs", "lws")
     load("S", T.vb[:, :], T.v[:, :], "vb", "lv")
 
+    LS = ["ls31", "lst", "ls8", "ls7", "ls6", "ls5", "ls4"]
+    E0 = ["e0.%d" % j for j in range(9)]
     op("G", lambda e: e.iota(T.pi[:, :], [[0, 1]], 0, 1), [], ["pi"])
+    iota(T.i512[:, 0:C], [[1, C]], 0, 0, ["i512"])
     iota(T.i16[:, :], [[0, 20], [1, 16]], 0, 0, ["i16"])
-    iota(T.i512[:, :], [[1, 512]], 0, 0, ["i512"])
+    iota(T.i512[:, C:512], [[1, 512 - C]], C, 0, ["i512b"])
     op("G", lambda e: e.iota(T.uli[:, :], [[16, 8]], 0, 0), [], ["uli"])
     vset(T.idt[:, :], 0.5, ["idt"])
-    vset(T.eb[:, :], 0.0, ["eb"])
-    vset(T.fc[:, :], 15.0, ["fc"])
-    vset(T.e0[:, :], 0.0, ["e0"])
-    vset(T.z8[:, :], 0.0, ["z8"])
     vset(T.yt[:, :], 0.0, ["yt0"])
-    vset(T.ls[:, :], 0, ["ls31", "lst", "ls8", "ls7", "ls6", "ls5", "ls4"])
+    vset(T.ls[:, :], 0, LS)
     vts(T.li[:, :], T.pi[:, :], 15, None, A.bitwise_and, None, ["pi"], ["li"])
+    vset(T.z8[:, :], 0.0, ["z8"])
     vcp(T.lf[:, :], T.li[:, :], ["li"], ["lf"])
     for j in range(4):
         vts(T.x4[:, j:j + 1], T.li[:, :], 8 >> j, None, A.bitwise_and, None, ["li"], ["x4%d" % j])
-    for j in range(4):
-        vts(T.bo[:, j:j + 1], T.x4[:, j:j + 1], float(40 << j), None, A.mult, None, ["x4%d" % j], ["bo%d" % j])
-    vcp(T.wo[:, 0:1], T.bo[:, 0:1], ["bo0"], ["wo0"])
-    vts(T.ma1[:, :], T.i16[:, :], T.lf[:, 0:1], None, A.is_equal, None, ["i16", "lf"], ["ma1"])
-    vts(T.d0r[:, :], T.i16[:, :], 0.0, None, A.not_equal, None, ["i16"], ["d0r"])
     vts(T.tr[:, :], T.lf[:, :], 0.0, 640.0, A.is_equal, A.mult, ["lf"], ["tr"])
-    act(T.dd[:, 0:C], T.i512[:, 0:C], ["i512"], ["dd"])
-    act(T.dd[:, C:2 * C], T.i512[:, 0:C], ["i512"], ["dd1"])
+    for j in range(4):
+        vts(T.bo[:, j:j + 1], T.x4[:, j:j + 1], 1.0 / (8 >> j), None, A.mult, None, ["x4%d" % j], ["bo%d" % j])
+    vset(T.fc[:, :], 15.0, ["fc%d" % j for j in range(14)])
+    vcp(T.wo[:, 0:1], T.bo[:, 0:1], ["bo0"], ["wo0"])
+    vset(T.e0[:, :], 0.0, E0)
+    vts(T.ma1[:, :], T.i16[:, :], T.lf[:, 0:1], None, A.is_equal, None, ["i16", "lf"], ["ma1"])
+    act(T.dd[:, 0:640:2], T.i512[:, 0:C], ["i512"], ["dd"])
+    act(T.dd[:, 1:640:2], T.i512[:, 0:C], ["i512"], ["dd1"])
+    act(T.d0r[:, :], T.i16[:, :], ["i16"], ["d0r"], F.Sign)
+    for b in range(4):
+        act(T.eb[:, 512 * b:512 * b + 512], T.i512[:, :], ["i512", "i512b"], ["eb%d" % b], scale=0.0)
     op("G", lambda e: e.affine_select(T.idt[:, :], T.idt[:, :], [[-1, 128]], A.is_equal, 0.0, 0, 1), ["idt"], ["idt"])
-    for j in range(4):
-        iota(T.fc[:, j:80:8], [[0, 10]], 271 + 16 * j, 0, ["fc"])
-    iota(T.fc[:, 20:80:8], [[0, 8]], 239, 0, ["fc"])
-    iota(T.fc[:, 21:80:8], [[0, 4], [16, 2]], 207, 0, ["fc"])
-    iota(T.fc[:, 22:80:8], [[0, 2], [16, 4]], 143, 0, ["fc"])
-    iota(T.fc[:, 23:80:8], [[16, 8]], 15, 0, ["fc"])
-    iota(T.fc[:, 96:104], [[8, 8]], 23, 0, ["fc"])
-    iota(T.fc[:, 104:112], [[1, 8]], 80, 0, ["fc"])
-    iota(T.fc[:, 112:120], [[8, 8]], 22, 0, ["fc"])
-    iota(T.fc[:, 120:124], [[8, 4]], 21, 0, ["fc"])
-    iota(T.fc[:, 124:126], [[8, 2]], 20, 0, ["fc"])
-    iota(T.fc[:, 126:128], [[-12, 2]], 19, 0, ["fc"])
-    iota(T.e0[:, 20:80:8], [[0, 4], [16, 2]], -8, 0, ["e0"])
-    iota(T.e0[:, 21:80:8], [[0, 2], [8, 2], [0, 2]], -4, 0, ["e0"])
-    iota(T.e0[:, 22:80:8], [[4, 2], [0, 4]], -2, 0, ["e0"])
-    iota(T.e0[:, 23:80:8], [[0, 8]], -1, 0, ["e0"])
     iota(T.i8[:, :], [[0, 10], [1, 8]], 0, 0, ["i8"])
-    iota(T.ji[:, :], [[16, 32]], 320, 1, ["ji"])
-
-    vts(T.si[:, :], T.sei[:, :], 1, None, A.bitwise_and, None, ["sei"], ["si"])
-    vts(T.ai[:, :], T.sei[:, :], 1, None, A.arith_shift_right, None, ["sei"], ["ai"])
-    vts(T.ci[:, :], T.si[:, :], 320.0, None, A.mult, None, ["si"], ["ci"])
-    vtt(T.oi[:, :], T.ci[:, :], T.ai[:, :], A.add, ["ci", "ai"], ["oi"])
-    vcp(T.ofl[:, 1:20], T.oi[:, 1:20], ["oi"], ["ofl"])
-    vts(T.ofl[:, 0:1], T.oi[:, 0:1], T.tr[:, 0:1], None, A.add, None, ["oi", "tr"], ["ofl0"])
-    vcp(T.dd[:, 0:656].indirect(T.ofl[:, 0:20]), T.i512[:, 0:C], ["ofl", "ofl0", "i512"], ["dd", "dd1"])
-    vcp(T.ull[:, :], T.uli[:, :], ["uli"], ["ull"])
-    vcp(T.parl[:, :], T.ai[:, :], ["ai"], ["parl"])
     for j in range(4):
-        vtt(T.g16[:, 16 * j:16 * j + 16], T.dd[:, 0:2 * C].indirect(T.wo[:, 2 * j:2 * j + 1]), T.ma1[:, 0:16], A.mult,
-            ["dd", "dd1", "wo%d" % j, "ma1"], ["g16%d" % j])
-        op("V", lambda e: e.tensor_reduce(T.yt[:, j + 1:j + 2], T.g16[:, 16 * j:16 * j + 16], AxisListType.X, A.add), ["g16%d" % j], ["yt%d" % (j + 1)])
-        if j < 3:
-            vts(T.wo[:, 2 * j + 2:2 * j + 3], T.yt[:, j + 1:j + 2], T.bo[:, j + 1:j + 2], None, A.add, None, ["yt%d" % (j + 1), "bo%d" % (j + 1)], ["wo%d" % (j + 1)])
-        else:
-            vcp(T.ls[:, 30:31], T.yt[:, 4:5], ["yt4"], ["ls4"])
-    vcp(T.ls[:, 32:36], T.yt[:, 0:4], ["yt0", "yt1", "yt2", "yt3"], ["lst"])
+        iota(T.fc[:, j:80:8], [[0, 10]], 271 + 16 * j, 0, ["fc%d" % j])
+    iota(T.fc[:, 20:80:8], [[0, 8]], 239, 0, ["fc4"])
+    iota(T.fc[:, 21:80:8], [[0, 4], [16, 2]], 207, 0, ["fc5"])
+    iota(T.fc[:, 22:80:8], [[0, 2], [16, 4]], 143, 0, ["fc6"])
+    iota(T.fc[:, 23:80:8], [[16, 8]], 15, 0, ["fc7"])
+    iota(T.fc[:, 96:104], [[8, 8]], 23, 0, ["fc8"])
+    iota(T.fc[:, 104:112], [[1, 8]], 80, 0, ["fc9"])
+    iota(T.fc[:, 112:120], [[8, 8]], 22, 0, ["fc10"])
+    iota(T.fc[:, 120:124], [[8, 4]], 21, 0, ["fc11"])
+    iota(T.fc[:, 124:126], [[8, 2]], 20, 0, ["fc12"])
+    iota(T.fc[:, 126:128], [[-12, 2]], 19, 0, ["fc13"])
+    iota(T.e0[:, 20:80:8], [[0, 4], [16, 2]], -8, 0, ["e0.4"])
+    iota(T.e0[:, 21:80:8], [[0, 2], [8, 2], [0, 2]], -4, 0, ["e0.5"])
+    iota(T.e0[:, 22:80:8], [[4, 2], [0, 4]], -2, 0, ["e0.6"])
+    iota(T.e0[:, 23:80:8], [[0, 8]], -1, 0, ["e0.7"])
+    iota(T.ji[:, :], [[16, 32]], 320, 1, ["ji"])
+    act(T.ma2[:, :], T.ma1[:, :], ["ma1"], ["ma2"], scale=2.0)
+    act(T.d0l[:, :], T.ma1[:, :], ["ma1"], ["d0l"], F.Identity, bias=1024.0, scale=-66560.0)
+    act(T.d0t[:, :], T.i8[:, :], ["i8"], ["d0t"], F.Sign)
+    for b in range(4):
+        act(T.eb[:, 512 * b + b:512 * b + 512:4], T.idt[:, :], ["idt"], ["eb%d" % b])
 
-    quant(T.q0[:, 0:C], T.qs0[:, 0:C], T.x0[:, 0:1280], ["x0"], ["q0"])
-    quant(T.uq[:, :], T.us[:, :], T.ub[:, :], ["ub"], ["uq"])
-    vcp(T.ur[:, 0:128].bitcast(dt.uint32), T.uq[:, 0:128].bitcast(dt.uint32).indirect(T.ull[:, 0:8]), ["uq", "ull"], ["ur"])
-    act(T.urs[:, 0:128], T.us[:, 0:128].indirect(T.ull[:, 0:8]), ["uq", "ull"], ["urs"])
-
-    for n, s0, s1, a, b in ((1, 30, 28, "ls4", "ls5"), (2, 28, 24, "ls5", "ls6"), (4, 24, 16, "ls6", "ls7"), (8, 16, 0, "ls7", "ls8")):
-        k = 16 * n
-        if n == 8:
-            vts(T.ma2[:, :], T.ma1[:, :], 2.0, None, A.mult, None, ["ma1"], ["ma2"])
-        vtt(T.gg[:, 0:k], T.dd[:, 0:C].indirect(T.ls[:, s0:s0 + n]), T.ma1[:, 0:k], A.mult, ["dd", a, "ma1"], ["gga"])
-        vtt(T.gg[:, k:2 * k], T.dd[:, C:2 * C].indirect(T.ls[:, s0:s0 + n]), T.ma1[:, 0:k], A.mult, ["dd1", a, "ma1"], ["ggb"])
-        vscan(T.gs[:, 0:2 * k], T.d0r[:, 0:2 * k], T.gg[:, 0:2 * k], 0.0, A.mult, A.add, ["gga", "ggb", "d0r"], ["gs"])
-        vcp(T.ls[:, s1:s1 + 2 * n], T.gs[:, 15:2 * k:16], ["gs"], [b])
+    vts(T.ofl[:, 0:1], T.sei[:, 0:1], T.tr[:, 0:1], None, A.add, None, ["sei", "tr"], ["ofl0"])
+    vcp(T.ofl[:, 1:20], T.sei[:, 1:20], ["sei"], ["ofl"])
+    vcp(T.dd[:, 0:656].indirect(T.ofl[:, 0:20]), T.i512[:, 0:C], ["ofl", "ofl0", "i512"], ["dd", "dd1"])
+    later(vcp, T.ull[:, :], T.uli[:, :], ["uli"], ["ull"])
+    later(vts, T.ai[:, :], T.sei[:, :], 1, None, A.arith_shift_right, None, ["sei"], ["ai"])
+    later(vset, T.t4[:, :], 0, ["t4%d" % j for j in range(4)])
+    later(vcp, T.parl[:, :], T.ai[:, :], ["ai"], ["parl"])
     for j in range(3):
-        vts(T.t4[:, j:j + 1], T.li[:, :], 7 >> j, None, A.bitwise_and, None, ["li"], ["t4"])
-    vset(T.t4[:, 3:4], 0, ["t4"])
-    vts(T.m4[:, :], T.t4[:, :], 0.0, None, A.not_equal, None, ["t4"], ["m4"])
-    vtt(T.oh[:, 0:3], T.m4[:, 0:3], T.m4[:, 1:4], A.subtract, ["m4"], ["oh"])
-    vtt(T.yo[:, 0:3], T.yt[:, 1:4], T.oh[:, 0:3], A.mult, ["oh", "yt1", "yt2", "yt3"], ["yo"])
-    op("V", lambda e: e.tensor_reduce(T.yo[:, 4:5], T.yo[:, 0:3], AxisListType.X, A.add), ["yo"], ["yo4"])
-    vcp(T.ls[:, 31:32], T.yo[:, 4:5], ["yo4"], ["ls31"])
-    LS = ["ls31", "lst", "ls8", "ls7", "ls6", "ls5", "ls4"]
+        later(vts, T.t4[:, j:j + 1], T.li[:, :], 7 >> j, None, A.bitwise_and, None, ["li"], ["t4%d" % j])
+    for j in range(4):
+        later(vts, T.w4[:, j:j + 1], T.x4[:, j:j + 1], 32.0, float(-(128 >> j)), A.mult, A.add, ["x4%d" % j], ["w4%d" % j])
+    later(vts, T.m8[:, :], T.t4[:, :], 0.0, None, A.not_equal, None, ["t4%d" % j for j in range(4)], ["m8"])
+    for j in range(4):
+        later(vts, T.e0[:, 16 + j:80:8], T.z8[:, :], T.w4[:, j:j + 1], None, A.add, None, ["z8", "w4%d" % j], ["e0.%d" % j])
+    later(vtt, T.e0[:, 0:4], T.w4[:, :], T.m8[:, 0:4], A.mult, ["w40", "w41", "w42", "w43", "m8"], ["e0.8"])
+    later(vtt, T.oh[:, 0:3], T.m8[:, 0:3], T.m8[:, 1:4], A.subtract, ["m8"], ["oh"])
+    later(vts, T.fl0[:, :], T.lf[:, :], 0.0, None, A.is_equal, None, ["lf"], ["fl0"])
+    later(vset, T.d0t[:, 0:1], 1.0, ["d0t"])
+    later(vts, T.subl[:, :], T.lf[:, :], -1024.0, 15360.0, A.mult, A.add, ["lf"], ["subl"])
+    later(vts, T.ini[:, :], T.fl0[:, :], -256.0, None, A.mult, None, ["fl0"], ["ini"])
+    later(vtt, T.yo[:, 0:3], T.yt[:, 1:4], T.oh[:, 0:3], A.mult, ["oh", "yt1", "yt2", "yt3"], ["yo"])
+    later(vcp, T.ls[:, 32:36], T.yt[:, 0:4], ["yt0", "yt1", "yt2", "yt3"], ["lst"])
+    later(vred, T.yo[:, 4:5], T.yo[:, 0:3], ["yo"], ["yo4"])
+    later(vtt, T.fm[:, :], T.fc[:, :], T.ma1[:, 0:128], A.mult, ["fc%d" % j for j in range(14)] + ["ma1"], ["fm"])
+    later(vcp, T.ls[:, 31:32], T.yo[:, 4:5], ["yo4"], ["ls31"])
+    later(vscan, T.fs[:, :], T.d0r[:, 0:128], T.fm[:, :], 0.0, A.mult, A.add, ["fm", "d0r"], ["fs"])
+    later(vcp, T.tl[:, 0:8], T.fs[:, 15:128:16], ["fs"], ["tl"])
+
+    for j in range(4):
+        vtt(T.g16[:, 16 * j:16 * j + 16], T.dd[:, 0:640].indirect(T.wo[:, 2 * j:2 * j + 1]), T.ma1[:, 0:16], A.mult,
+            ["dd", "dd1", "wo%d" % j, "ma1"], ["g16%d" % j])
+        fill()
+        vred(T.yt[:, j + 1:j + 2], T.g16[:, 16 * j:16 * j + 16], ["g16%d" % j], ["yt%d" % (j + 1)])
+        fill()
+        y = T.yt[:, j + 1:j + 2]
+        if j < 3:
+            vts(T.wo[:, 2 * j + 2:2 * j + 3], y, 2.0, T.bo[:, j + 1:j + 2], A.mult, A.add, ["yt%d" % (j + 1), "bo%d" % (j + 1)], ["wo%d" % (j + 1)])
+        else:
+            vts(T.wv[:, 0:1], y, 2.0, None, A.mult, None, ["yt4"], ["wv0"])
+            vts(T.wv[:, 1:2], y, 2.0, 1.0, A.mult, A.add, ["yt4"], ["wv1"])
+            vcp(T.ls[:, 30:31], y, ["yt4"], ["ls4"])
+        fill()
+
+    for n, s1, b, o, o1 in ((1, 28, "ls5", 0, 2), (2, 24, "ls6", 2, 6), (4, 16, "ls7", 6, 14), (8, 0, "ls8", 14, 0)):
+        k, h = 32 * n, 32 * (n - 1)
+        vtt(T.gg[:, h:h + k], T.dd[:, 0:640].indirect(T.wv[:, o:o + 2 * n]), T.ma1[:, 0:k], A.mult, ["dd", "dd1", "wv0", "wv1", "ma1"], [b + "g"])
+        if n == 1:
+            quant(T.uq[:, :], T.us[:, :], T.ub[:, :], ["ub"], ["uq"])
+        else: fill()
+        vscan(T.gs[:, h:h + k], T.d0r[:, 0:k], T.gg[:, h:h + k], 0.0, A.mult, A.add, [b + "g", "d0r"], [b + "s"])
+        if n == 1:
+            vcp(T.ur[:, 0:128].bitcast(dt.uint32), T.uq[:, 0:128].bitcast(dt.uint32).indirect(T.ull[:, 0:8]), ["uq", "ull"], ["ur"])
+            act(T.urs[:, 0:128], T.us[:, 0:128].indirect(T.ull[:, 0:8]), ["uq", "ull"], ["urs"])
+        elif n == 2:
+            quant(T.q0[:, 0:C], T.qs0[:, 0:C], T.x0[:, 0:1280], ["x0"], ["q0"])
+        else: fill()
+        y = T.gs[:, h + 15:h + k:16]
+        if n < 8:
+            vts(T.wv[:, o1:o1 + 2 * n], y, 2.0, None, A.mult, None, [b + "s"], ["wv0"])
+            vts(T.wv[:, o1 + 2 * n:o1 + 4 * n], y, 2.0, 1.0, A.mult, A.add, [b + "s"], ["wv1"])
+        vcp(T.ls[:, s1:s1 + 2 * n], y, [b + "s"], [b])
+        fill()
+    fill(len(spare))
 
     def labels(k):
         send(T.ll[:, 32 * k:32 * k + 32], T.ls[:, 0:32], "lb%d" % k, partner[k], LS)
 
     labels(0)
 
-    for j in range(4):
-        vts(T.w4[:, j:j + 1], T.x4[:, j:j + 1], 32.0, float(-(128 >> j)), A.mult, A.add, ["x4%d" % j], ["w4"])
-    for j in range(4):
-        vts(T.e0[:, 16 + j:80:8], T.z8[:, :], T.w4[:, j:j + 1], None, A.add, None, ["z8", "w4"], ["e0"])
-    vtt(T.e0[:, 0:4], T.w4[:, :], T.m4[:, :], A.mult, ["w4", "m4"], ["e0"])
-    vts(T.fl0[:, :], T.lf[:, :], 0.0, None, A.is_equal, None, ["lf"], ["fl0"])
-    vts(T.ini[:, :], T.fl0[:, :], -256.0, None, A.mult, None, ["fl0"], ["ini"])
-    vts(T.d0t[:, :], T.i8[:, :], 0.0, None, A.not_equal, None, ["i8"], ["d0t"])
-    vset(T.d0t[:, 0:1], 1.0, ["d0t"])
-    vtt(T.fm[:, :], T.fc[:, :], T.ma1[:, 0:128], A.mult, ["fc", "ma1"], ["fm"])
-    vscan(T.fs[:, :], T.d0r[:, 0:128], T.fm[:, :], 0.0, A.mult, A.add, ["fm", "d0r"], ["fs"])
-    vcp(T.tl[:, 0:8], T.fs[:, 15:128:16], ["fs"], ["tl"])
+    later(vcp, T.yf[:, :], T.ls[:, :], LS, ["yf"])
+    later(vts, T.tls[:, 0:5], T.fs[:, 15:80:16], 0.0625, 15.0625, A.mult, A.add, ["fs"], ["tls"])
+    later(vtt, T.y32[:, :], T.yf[:, 0:32], T.ji[:, :], A.subtract, ["yf", "ji"], ["y32"])
+    later(vcp, T.lab[:, :], T.yf[:, 0:36].indirect(T.tls[:, 0:5]), ["yf", "tls"], ["lab"])
+    later(vtt, T.eqv[:, 0:79], T.lab[:, 1:80], T.lab[:, 0:79], A.is_equal, ["lab"], ["eqv"])
+    later(vtt, T.eqr[:, :], T.lab[:, 23:80:8], T.yf[:, 8:16], A.is_equal, ["lab", "yf"], ["eqr"])
+    later(vtt, T.eqv[:, 23:80:8], T.lab[:, 23:80:8], T.yf[:, 0:8], A.is_equal, ["lab", "yf"], ["eqv"])
+    later(vtt, T.eqv[:, 0:8], T.eqv[:, 0:8], T.m8[:, :], A.mult, ["eqv", "m8"], ["eqv"])
+    later(vscan, T.cs[:, 0:80], T.d0t[:, :], T.eqv[:, :], T.fl0[:, 0:1], A.mult, A.add, ["eqv", "d0t", "fl0"], ["cs"])
+    later(vtt, T.cs[:, 80:88], T.cs[:, 22:80:8], T.eqr[:, :], A.add, ["cs", "eqr"], ["csr"])
+    later(vts, T.z32[:, :], T.cs[:, 0:88].indirect(T.tl[:, 6:8]), 0.0, None, A.is_equal, None, ["cs", "csr", "tl"], ["z32"])
+    later(vtt, T.zy[:, :], T.z32[:, :], T.y32[:, :], A.mult, ["z32", "y32"], ["zy"])
+    later(vtt, T.o32[:, :], T.zy[:, :], T.ji[:, :], A.add, ["zy", "ji"], ["o32"])
+    later(vcp, T.ol[:, :], T.o32[:, :], ["o32"], ["ol"])
 
-    ee = ["e0", "e1"]
     for r in range(3):
         q, qs, qt = T["q%d" % r], T["qs%d" % r], "q%d" % r
         Q, QS = q[:, 0:C], qs[:, 0:C]
@@ -260,71 +281,61 @@ def rank_program(g, core, T, topo):
         for b in range(4):
             mm(1 + b, T.wq[:, 128 * b:128 * b + 128], T.wqs[:, 128 * b:128 * b + 128], Q, QS, [qt, "wq", "wqs"])
         vts(T.tb[:, :], bank(0), 0.0, 0.5, A.is_ge, A.subtract, ["bank0"], ["tb"])
+        fill()
         vtt(T.mg[:, :], T.tb[:, 0:C].indirect(T.ls[:, 16:36]), T.ma2[:, :], A.mult, ["tb", "ma2"] + LS, ["mg"])
+        fill()
         vscan(T.sc[:, :], T.d0r[:, :], T.mg[:, :], 0.0, A.mult, A.add, ["mg", "d0r"], ["sc"])
-        eo, en = ee[r % 2], ee[(r + 1) % 2]
-        vtt(T[en][:, :], T.sc[:, 0:C].indirect(T.tl[:, 0:5]), T[eo][:, :], A.mult, ["sc", "tl", eo], [en])
-        vscan(T.pp[:, 0:80], T.d0t[:, :], T[en][:, :], T.ini[:, 0:1], A.mult, A.add, [en, "d0t", "ini"], ["pp"])
-        vtt(T.pp[:, 80:88], T.pp[:, 22:80:8], T[en][:, 23:80:8], A.subtract, ["pp", en], ["ppr"])
+        fill()
+        eo, en, te, tn = (T.e0, T.e1, E0, ["e1"]) if r % 2 == 0 else (T.e1, T.e0, ["e1"], E0)
+        vtt(en[:, :], T.sc[:, 0:C].indirect(T.tl[:, 0:5]), eo[:, :], A.mult, ["sc", "tl"] + te, tn)
+        fill()
+        vscan(T.pp[:, 0:80], T.d0t[:, :], en[:, :], T.ini[:, 0:1], A.mult, A.add, tn + ["d0t", "ini"], ["pp"])
+        fill()
+        vtt(T.pp[:, 80:88], T.pp[:, 22:80:8], en[:, 23:80:8], A.subtract, ["pp"] + tn, ["ppr"])
+        fill()
         pl, pa = T.pl[:, 32 * r:32 * r + 32], T.pa[:, 32 * r:32 * r + 32]
         vts(pl, T.pp[:, 0:88].indirect(T.tl[:, 6:8]), 256.0, None, A.add, None, ["pp", "ppr", "tl"], ["pl%d" % r])
         send(pa, pl, "pr%d" % r, partner[r], ["pl%d" % r])
+        fill()
         hb = T["hb%d" % r]
         for b in range(4):
             act(hb[:, b:1280:4], bank(1 + b), ["bank%d" % (1 + b)], ["hb%d.%d" % (r, b)], scale=0.03125)
         quant(T["hq%d" % r][:, 0:C], T["hs%d" % r][:, 0:C], hb[:, 0:1280], ["hb%d.%d" % (r, b) for b in range(4)], ["hq%d" % r])
         send(T["lq%d" % r][:, 0:C].bitcast(dt.uint8), T["hq%d" % r][:, 0:C].bitcast(dt.uint8), "cr%d" % r, partner[r], ["hq%d" % r])
         send(T["lqs%d" % r][:, 0:C], T["hs%d" % r][:, 0:C], "sr%d" % r, partner[r], ["hq%d" % r])
+        fill()
         if r == 0:
             labels(1)
             labels(2)
-            for b in range(4):
-                vcp(T.eb[:, 512 * b + b:512 * b + 512:4], T.idt[:, :], ["idt", "eb"], ["eb%d" % b])
             quant(T.eq[:, :], T.es[:, :], T.eb[:, :], ["eb0", "eb1", "eb2", "eb3"], ["eq"])
         fb = [5, 6, 7, 0]
         for b in range(4):
             mm(fb[b], T.eq[:, 128 * b:128 * b + 128], T.es[:, 128 * b:128 * b + 128], Q, QS, [qt, "eq"])
+        act(T.prep[:, :], T.i512[:, :].indirect(pl), ["i512", "i512b", "pl%d" % r], ["prep"])
         if r == 0:
-            vts(T.la[:, :], T.i16[:, :], T.lf[:, 0:1], None, A.subtract, None, ["i16", "lf"], ["la"])
-            vts(T.lb[:, :], T.la[:, :], 0.0, -65536.0, A.is_equal, A.mult, ["la"], ["lb"])
-            vts(T.la[:, :], T.la[:, :], 1.0, 1024.0, A.is_equal, A.mult, ["la", "lb"], ["la"])
-            vtt(T.d0l[:, :], T.la[:, :], T.lb[:, :], A.add, ["la", "lb"], ["d0l"])
-            vts(T.subl[:, :], T.lf[:, :], 15.0, 1024.0, A.not_equal, A.mult, ["lf"], ["subl"])
-            vts(T.tls[:, 0:5], T.fs[:, 15:80:16], 0.0625, 15.0625, A.mult, A.add, ["fs"], ["tls"])
-            vcp(T.yf[:, :], T.ls[:, :], LS, ["yf"])
-            vcp(T.lab[:, :], T.yf[:, 0:36].indirect(T.tls[:, 0:5]), ["yf", "tls"], ["lab"])
-            vset(T.eqv[:, :], 0.0, ["eqv"])
-            vtt(T.eqv[:, 0:79], T.lab[:, 1:80], T.lab[:, 0:79], A.is_equal, ["lab"], ["eqv"])
-            vtt(T.eqv[:, 23:80:8], T.lab[:, 23:80:8], T.yf[:, 0:8], A.is_equal, ["lab", "yf"], ["eqv"])
-            vtt(T.eqr[:, :], T.lab[:, 23:80:8], T.yf[:, 8:16], A.is_equal, ["lab", "yf"], ["eqr"])
-            vtt(T.eqv[:, 0:4], T.eqv[:, 0:4], T.m4[:, :], A.mult, ["eqv", "m4"], ["eqv"])
-            vset(T.eqv[:, 4:8], 0.0, ["eqv"])
-            vscan(T.cs[:, 0:80], T.d0t[:, :], T.eqv[:, :], T.fl0[:, 0:1], A.mult, A.add, ["eqv", "d0t", "fl0"], ["cs"])
-            vtt(T.cs[:, 80:88], T.cs[:, 22:80:8], T.eqr[:, :], A.add, ["cs", "eqr"], ["csr"])
-            vcp(T.c32[:, :], T.cs[:, 0:88].indirect(T.tl[:, 6:8]), ["cs", "csr", "tl"], ["c32"])
-            vts(T.z32[:, :], T.c32[:, :], 0.0, None, A.is_equal, None, ["c32"], ["z32"])
-            vts(T.n32[:, :], T.c32[:, :], 0.0, None, A.is_gt, None, ["c32"], ["n32"])
-            vtt(T.a32[:, :], T.z32[:, :], T.yf[:, 0:32], A.mult, ["z32", "yf"], ["a32"])
-            vtt(T.b32[:, :], T.n32[:, :], T.ji[:, :], A.mult, ["n32", "ji"], ["b32"])
-            vtt(T.o32[:, :], T.a32[:, :], T.b32[:, :], A.add, ["a32", "b32"], ["o32"])
-            vcp(T.ol[:, :], T.o32[:, :], ["o32"], ["ol"])
-            vcp(T.at[:, 0:960].indirect(T.ol[:, 0:32]), T.i512[:, :], ["ol", "i512"], ["at"])
+            for b in range(4):
+                act(T.fw[:, C * b:C * b + C], bank(fb[b]), ["bank%d" % fb[b]], ["fw%d" % b])
+            fill(len(spare))
+            vcp(T.at[:, 0:960].indirect(T.ol[:, 0:32]), T.i512[:, :], ["ol", "i512", "i512b"], ["at"])
             vscan(T.als[:, :], T.d0l[:, :], T.at[:, 0:C], 0.0, A.add, A.max, ["at", "d0l"], ["als"])
             vts(T.al[:, :], T.als[:, 15:C:16], T.subl[:, 0:1], None, A.subtract, None, ["als", "subl"], ["al"])
-        act(T.prep[:, :], T.i512[:, :].indirect(pl), ["i512", "pl%d" % r], ["prep"])
-        act(T.brep[:, :], T.prep[:, :].indirect(T.al[:, 0:20]), ["prep", "al"], ["brep"])
-        for b in range(4):
-            vcp(T.fw[:, C * b:C * b + C], bank(fb[b]), ["bank%d" % fb[b]], ["fw%d" % b])
-        vscan(T.bsc[:, :], T.d0l[:, :], T.brep[:, :], 0.0, A.add, A.max, ["brep", "d0l"], ["bsc"])
-        vts(T.bl[:, :], T.bsc[:, 15:C:16], T.subl[:, 0:1], None, A.subtract, None, ["bsc", "subl"], ["bl"])
-        if r == 0:
             lastw["ll0"] = ("lb0", len(topo.engines(core, partner[0])))
             act(T.lr[:, 0:512], T.i512[:, 0:C].indirect(T.ll[:, 0:32]), ["i512", "ll0"], ["lr0"])
-        for b in range(4):
-            act(T.fg[:, C * b:C * b + C], T.fw[:, C * b:C * b + C].indirect(T.parl[:, 0:20]), ["fw%d" % b, "parl"], ["fg%d" % b])
+            for b in range(4):
+                act(T.fg[:, C * b:C * b + C], T.fw[:, C * b:C * b + C].indirect(T.parl[:, 0:20]), ["fw%d" % b, "parl"], ["fg%d" % b])
+        act(T.brep[:, :], T.prep[:, :].indirect(T.al[:, 0:20]), ["prep", "al"], ["brep"])
+        if r:
+            for b in range(4):
+                vcp(T.fw[:, C * b:C * b + C], bank(fb[b]), ["bank%d" % fb[b]], ["fw%d" % b])
+            for b in range(4):
+                act(T.fg[:, C * b:C * b + C], T.fw[:, C * b:C * b + C].indirect(T.parl[:, 0:20]), ["fw%d" % b, "parl"], ["fg%d" % b])
         k = len(topo.engines(core, partner[r]))
         lastw["pa%d" % r], lastw["lq%d" % r], lastw["lqs%d" % r] = ("pr%d" % r, k), ("cr%d" % r, k), ("sr%d" % r, k)
-        vcp(T.zt[:, :].indirect(pa), T.lr[:, 512 * r:512 * r + 512], ["pa%d" % r, "lr%d" % r], ["zt"])
+        zt = (T.zt[:, :].indirect(pa), T.lr[:, 512 * r:512 * r + 512], ["pa%d" % r, "lr%d" % r], ["zt"])
+        if r == 0: vcp(*zt)
+        vscan(T.bsc[:, :], T.d0l[:, :], T.brep[:, :], 0.0, A.add, A.max, ["brep", "d0l"], ["bsc"])
+        vts(T.bl[:, :], T.bsc[:, 15:C:16], T.subl[:, 0:1], None, A.subtract, None, ["bsc", "subl"], ["bl"])
+        if r: vcp(*zt)
         vcp(T.mr[:, :], T.zt[:, :].indirect(T.bl[:, 0:20]), ["zt", "bl"], ["mr"])
         vscan(T.msc[:, :], T.d0l[:, :], T.mr[:, :], 0.0, A.add, A.max, ["mr", "d0l"], ["msc"])
         vts(T.ml[:, :], T.msc[:, 15:C:16], T.subl[:, 0:1], None, A.subtract, None, ["msc", "subl"], ["ml"])

@@ -3,6 +3,7 @@ from concourse.mybir import dt, AluOpType, AxisListType, ActivationFunctionType
 
 C = 320
 STEP = [1, 2, 4]
+PARTS = [(0, 192), (192, 320)]
 A = AluOpType
 F = ActivationFunctionType
 
@@ -14,40 +15,67 @@ for _n, _w, _d in (
         ("idt", 128, "bfloat16"), ("eb", 2048, "bfloat16"), ("eq", 512, "float8_e4m3fn_x4"), ("es", 512, "uint8"),
         ("pi", 1, "int32"), ("li", 1, "int32"), ("lf", 1, "float32"), ("i16", 320, "float32"), ("i512", 512, "float32"),
         ("ma1", 320, "bfloat16"), ("ma2", 320, "bfloat16"), ("d0r", 320, "bfloat16"), ("d0l", 320, "float32"),
-        ("subl", 1, "float32"), ("i8", 80, "float32"), ("d0t", 80, "float32"), ("x4", 4, "int32"), ("t4", 8, "int32"),
-        ("w4", 4, "float32"), ("bo", 4, "float32"), ("m8", 8, "float32"), ("oh", 4, "float32"), ("fl0", 1, "float32"),
-        ("ini", 1, "float32"), ("tr", 1, "float32"), ("z8", 8, "float32"), ("ji", 32, "float32"), ("fc", 128, "float32"),
-        ("fm", 128, "float32"), ("fs", 128, "float32"), ("tl", 8, "uint16"), ("tls", 6, "uint16"), ("uli", 8, "int32"), ("ull", 8, "uint16"),
+        ("subl", 1, "float32"), ("i8", 32, "float32"), ("d0t", 32, "float32"), ("x4", 4, "int32"), ("bo", 4, "float32"),
+        ("m4", 4, "float32"), ("oh", 4, "float32"), ("fl0", 1, "float32"), ("ini", 1, "float32"), ("tr", 1, "float32"),
+        ("zz", 16, "float32"), ("nd", 16, "float32"), ("ad", 16, "float32"), ("sg", 16, "float32"), ("an", 16, "float32"),
+        ("w1", 16, "float32"), ("w2", 16, "float32"), ("zl", 16, "float32"), ("zr", 1, "float32"), ("tm", 16, "float32"),
+        ("wt0", 16, "float32"), ("wt1", 16, "float32"), ("wm0", 16, "float32"), ("wm1", 16, "float32"), ("ba", 1, "float32"), ("bt", 1, "float32"),
+        ("ji", 32, "float32"), ("fc", 64, "float32"), ("fm", 64, "float32"), ("fs", 64, "float32"), ("tl", 4, "uint16"), ("tls", 2, "uint16"),
+        ("ull", 8, "uint16"),
         ("ai", 20, "int32"), ("ofl", 20, "uint16"), ("parl", 20, "uint16"), ("dd", 656, "float32"), ("wo", 8, "uint16"), ("wv", 32, "uint16"),
         ("g16", 64, "float32"), ("yt", 8, "float32"), ("yo", 8, "float32"), ("gg", 512, "float32"), ("gs", 512, "float32"),
-        ("ls", 36, "uint16"), ("yf", 36, "float32"), ("lab", 80, "float32"), ("eqv", 80, "float32"), ("eqr", 8, "float32"),
-        ("cs", 88, "float32"), ("z32", 32, "float32"), ("y32", 32, "float32"), ("zy", 32, "float32"), ("o32", 32, "float32"), ("ol", 32, "uint16"),
+        ("ls", 32, "uint16"), ("yf", 32, "float32"), ("lab", 32, "float32"), ("eqv", 32, "float32"), ("eqr", 8, "float32"),
+        ("eqp", 4, "float32"), ("eqm", 4, "float32"), ("cb", 1, "float32"), ("ct", 1, "float32"), ("cs", 42, "float32"), ("z32", 32, "float32"), ("y32", 32, "float32"), ("zy", 32, "float32"), ("o32", 32, "float32"), ("ol", 32, "uint16"),
         ("at", 960, "float32"), ("als", 320, "float32"), ("al", 20, "uint16"),
-        ("tb", 320, "bfloat16"), ("mg", 320, "bfloat16"), ("sc", 320, "bfloat16"), ("e0", 80, "float32"), ("e1", 80, "float32"),
-        ("pp", 88, "float32"), ("prep", 512, "float32"), ("brep", 320, "float32"), ("bsc", 320, "float32"), ("bl", 20, "uint16"),
+        ("tb", 320, "bfloat16"), ("mg", 256, "bfloat16"), ("sc", 240, "bfloat16"), ("e0", 32, "float32"), ("e1", 32, "float32"),
+        ("pp", 42, "float32"), ("prep", 512, "float32"), ("brep", 320, "float32"), ("bsc", 320, "float32"), ("bl", 20, "uint16"),
         ("zt", 512, "float32"), ("msc", 320, "float32"), ("ml", 20, "uint16"), ("mr", 320, "float32"), ("ysb", 320, "float32"),
         ("fw", 1280, "bfloat16"), ("fg", 1280, "bfloat16"), ("aw", 1280, "bfloat16"),
         ("pl", 96, "uint16"), ("pa", 96, "uint16"), ("ll", 96, "uint16"), ("lr", 1536, "float32")):
     SCRATCH[_n] = ("sbuf", [128, _w], _d)
-for _r in range(4):
+for _r in range(2):
     SCRATCH["q%d" % _r] = ("sbuf", [128, 320], "float8_e4m3fn_x4")
     SCRATCH["qs%d" % _r] = ("sbuf", [128, 320], "uint8")
+SCRATCH["xr"] = SCRATCH["hb"] = ("sbuf", [128, 1280], "bfloat16")
 for _r in range(3):
-    SCRATCH["xr%d" % _r] = ("sbuf", [128, 1280], "bfloat16")
-    SCRATCH["hb%d" % _r] = ("sbuf", [128, 1280], "bfloat16")
     SCRATCH["hq%d" % _r] = ("sbuf", [128, 320], "float8_e4m3fn_x4")
     SCRATCH["hs%d" % _r] = ("sbuf", [128, 320], "uint8")
     SCRATCH["lq%d" % _r] = ("sbuf", [128, 320], "float8_e4m3fn_x4")
     SCRATCH["lqs%d" % _r] = ("sbuf", [128, 320], "uint8")
 
-SEMAPHORES = ["cV", "cS", "cT", "cG", "sent", "stored", "lse", "lx", "lu", "lv", "lwc", "lws"]
+SEMAPHORES = ["cV", "cS", "cT", "cG", "sent", "stored", "hand", "handed", "sra", "lse", "lx", "lu", "lv", "lwc", "lws"]
 for _r in range(3):
     SEMAPHORES += ["pr%d" % _r, "lb%d" % _r, "cr%d" % _r, "sr%d" % _r]
+
+
+def relay_of(T, topo, rank, s):
+    core, dst = T.cores[rank], T.cores[rank ^ s]
+    if topo.chip(core) == topo.chip(dst): return None
+    mine = [c for c in topo.cores_of(core) if T.rank_of(c) is not None]
+    free = [c for c in topo.cores_of(core) if T.rank_of(c) is None and topo.die(c) != topo.die(core) and topo.may_write(c, dst)]
+    return free[mine.index(core) % len(free)]
+
+
+def hand_on(g, core, T, topo):
+    for rank in range(len(T.cores)):
+        for k, s in enumerate(STEP):
+            if relay_of(T, topo, rank, s) != core: continue
+            src, dst = T.cores[rank], T.cores[rank ^ s]
+            rid, pid, _s = topo.addr(dst)
+            m, n, got = topo.mask(core, dst), len(topo.engines(core, dst)), len(topo.engines(src, core))
+            c0, c1 = PARTS[0]
+            ll, hq, lq = T.ll[:, 32 * k:32 * k + 32], T["hq%d" % k][:, c0:c1].bitcast(dt.uint8), T["lq%d" % k][:, c0:c1].bitcast(dt.uint8)
+            g.wait_ge(T.sem["lb%d" % k], got)
+            g.remote_dma(ll, ll, T.sem["lb%d" % k], T.sem.sent, pid, rid, m)
+            g.wait_ge(T.sem.hand, got)
+            g.remote_dma(lq, hq, T.sem.handed, T.sem.sent, pid, rid, m)
+            g.wait_ge(T.sem.sent, 2 * n)
 
 
 def rank_program(g, core, T, topo):
     rank = T.rank_of(core)
     if rank is None:
+        hand_on(g, core, T, topo)
         return
     eng = {"V": g.vector, "S": g.scalar, "T": g.tensor, "G": g, "Y": g.sync}
     cnt = {"V": 0, "S": 0, "T": 0, "G": 0}
@@ -107,8 +135,8 @@ def rank_program(g, core, T, topo):
     def act(out, in_, r, w, f=F.Copy, **k): op("S", lambda e: e.activation(out, in_, f, **k), r, w)
     def quant(c, s, t, r, w): op("V", lambda e: e.quantize_mx(c, s, t), r, w)
 
-    def mm(bank, lc, lsc, rc, rsc, r):
-        out = T.ps[:, 512 * bank:512 * bank + C]
+    def mm(bank, lc, lsc, rc, rsc, r, n=C):
+        out = T.ps[:, 512 * bank:512 * bank + n]
         op("T", lambda e: e.matmul_mx(out, lc, lsc, rc, rsc, True, True), r, ["bank%d" % bank])
 
     def bank(b): return T.ps[:, 512 * b:512 * b + C]
@@ -123,13 +151,15 @@ def rank_program(g, core, T, topo):
 
     spare = []
 
-    def later(f, *a): spare.append(lambda: f(*a))
+    def later(f, *a, **k): spare.append(lambda: f(*a, **k))
 
     def fill(n=1):
         for _i in range(n):
             if spare: spare.pop(0)()
 
     partner = [T.cores[rank ^ s] for s in STEP]
+    relay = [relay_of(T, topo, rank, s) for s in STEP]
+    theirs = [relay_of(T, topo, rank ^ s, s) for s in STEP]
 
     load("Y", T.sei[:, :], T.se[:, :], "sei", "lse")
     load("S", T.ub[:, :], T.u[:, :], "ub", "lu")
@@ -138,27 +168,31 @@ def rank_program(g, core, T, topo):
     load("Y", T.wqs[:, :], T.ws[:, :], "wqs", "lws")
     load("S", T.vb[:, :], T.v[:, :], "vb", "lv")
 
-    LS = ["ls31", "lst", "ls8", "ls7", "ls6", "ls5", "ls4"]
-    E0 = ["e0.%d" % j for j in range(9)]
+    LS = ["ls31", "ls8", "ls7", "ls6", "ls5", "ls4"]
+    E0 = ["e0.%d" % j for j in range(4)]
+    FC = ["fc%d" % j for j in range(10)]
+    ZZ = ["zz%d" % j for j in range(5)]
     op("G", lambda e: e.iota(T.pi[:, :], [[0, 1]], 0, 1), [], ["pi"])
     iota(T.i512[:, 0:C], [[1, C]], 0, 0, ["i512"])
     iota(T.i16[:, :], [[0, 20], [1, 16]], 0, 0, ["i16"])
     iota(T.i512[:, C:512], [[1, 512 - C]], C, 0, ["i512b"])
-    op("G", lambda e: e.iota(T.uli[:, :], [[16, 8]], 0, 0), [], ["uli"])
     vset(T.idt[:, :], 0.5, ["idt"])
     vset(T.yt[:, :], 0.0, ["yt0"])
     vset(T.ls[:, :], 0, LS)
     vts(T.li[:, :], T.pi[:, :], 15, None, A.bitwise_and, None, ["pi"], ["li"])
-    vset(T.z8[:, :], 0.0, ["z8"])
+    vset(T.m4[:, :], 0.0, ["m0", "m1", "m2", "m3"])
     vcp(T.lf[:, :], T.li[:, :], ["li"], ["lf"])
     for j in range(4):
         vts(T.x4[:, j:j + 1], T.li[:, :], 8 >> j, None, A.bitwise_and, None, ["li"], ["x4%d" % j])
     vts(T.tr[:, :], T.lf[:, :], 0.0, 640.0, A.is_equal, A.mult, ["lf"], ["tr"])
     for j in range(4):
         vts(T.bo[:, j:j + 1], T.x4[:, j:j + 1], 1.0 / (8 >> j), None, A.mult, None, ["x4%d" % j], ["bo%d" % j])
-    vset(T.fc[:, :], 15.0, ["fc%d" % j for j in range(14)])
+    vset(T.ma2[:, 240:256], 2.0, ["ma2b"])
     vcp(T.wo[:, 0:1], T.bo[:, 0:1], ["bo0"], ["wo0"])
-    vset(T.e0[:, :], 0.0, E0)
+    vset(T.pp[:, 40:41], 0.0, ["pp0"])
+    vset(T.cs[:, 40:41], 0.0, ["cs0"])
+    vts(T.fl0[:, :], T.lf[:, :], 0.0, None, A.is_equal, None, ["lf"], ["fl0"])
+    vts(T.nd[:, :], T.i16[:, 0:16], T.lf[:, 0:1], None, A.subtract, None, ["i16", "lf"], ["nd"])
     vts(T.ma1[:, :], T.i16[:, :], T.lf[:, 0:1], None, A.is_equal, None, ["i16", "lf"], ["ma1"])
     act(T.dd[:, 0:640:2], T.i512[:, 0:C], ["i512"], ["dd"])
     act(T.dd[:, 1:640:2], T.i512[:, 0:C], ["i512"], ["dd1"])
@@ -166,25 +200,34 @@ def rank_program(g, core, T, topo):
     for b in range(4):
         act(T.eb[:, 512 * b:512 * b + 512], T.i512[:, :], ["i512", "i512b"], ["eb%d" % b], scale=0.0)
     op("G", lambda e: e.affine_select(T.idt[:, :], T.idt[:, :], [[-1, 128]], A.is_equal, 0.0, 0, 1), ["idt"], ["idt"])
-    iota(T.i8[:, :], [[0, 10], [1, 8]], 0, 0, ["i8"])
-    for j in range(4):
-        iota(T.fc[:, j:80:8], [[0, 10]], 271 + 16 * j, 0, ["fc%d" % j])
-    iota(T.fc[:, 20:80:8], [[0, 8]], 239, 0, ["fc4"])
-    iota(T.fc[:, 21:80:8], [[0, 4], [16, 2]], 207, 0, ["fc5"])
-    iota(T.fc[:, 22:80:8], [[0, 2], [16, 4]], 143, 0, ["fc6"])
-    iota(T.fc[:, 23:80:8], [[16, 8]], 15, 0, ["fc7"])
-    iota(T.fc[:, 96:104], [[8, 8]], 23, 0, ["fc8"])
-    iota(T.fc[:, 104:112], [[1, 8]], 80, 0, ["fc9"])
-    iota(T.fc[:, 112:120], [[8, 8]], 22, 0, ["fc10"])
-    iota(T.fc[:, 120:124], [[8, 4]], 21, 0, ["fc11"])
-    iota(T.fc[:, 124:126], [[8, 2]], 20, 0, ["fc12"])
-    iota(T.fc[:, 126:128], [[-12, 2]], 19, 0, ["fc13"])
-    iota(T.e0[:, 20:80:8], [[0, 4], [16, 2]], -8, 0, ["e0.4"])
-    iota(T.e0[:, 21:80:8], [[0, 2], [8, 2], [0, 2]], -4, 0, ["e0.5"])
-    iota(T.e0[:, 22:80:8], [[4, 2], [0, 4]], -2, 0, ["e0.6"])
-    iota(T.e0[:, 23:80:8], [[0, 8]], -1, 0, ["e0.7"])
+    iota(T.zz[:, 1:16:2], [[0, 8]], 1, 0, ["zz0"])
+    iota(T.zz[:, 2:16:4], [[0, 4]], 2, 0, ["zz1"])
+    iota(T.zz[:, 4:16:8], [[0, 2]], 4, 0, ["zz2"])
+    iota(T.zz[:, 8:9], [[0, 1]], 8, 0, ["zz3"])
+    iota(T.zz[:, 0:1], [[0, 1]], 16, 0, ["zz4"])
+    iota(T.i8[:, :], [[0, 8], [1, 4]], 0, 0, ["i8"])
+    iota(T.fc[:, 0:32:4], [[0, 8]], 239, 0, ["fc0"])
+    iota(T.fc[:, 1:32:4], [[0, 4], [16, 2]], 207, 0, ["fc1"])
+    iota(T.fc[:, 2:32:4], [[0, 2], [16, 4]], 143, 0, ["fc2"])
+    iota(T.fc[:, 3:32:4], [[16, 8]], 15, 0, ["fc3"])
+    iota(T.fc[:, 32:40], [[4, 8]], 3, 0, ["fc4"])
+    iota(T.fc[:, 40:48], [[1, 8]], 32, 0, ["fc5"])
+    iota(T.fc[:, 48:56], [[4, 8]], 2, 0, ["fc6"])
+    iota(T.fc[:, 56:60], [[4, 4]], 1, 0, ["fc7"])
+    iota(T.fc[:, 60:62], [[4, 2]], 0, 0, ["fc8"])
+    iota(T.fc[:, 62:64], [[1, 2]], 40, 0, ["fc9"])
+    iota(T.e0[:, 0:32:4], [[0, 4], [16, 2]], -8, 0, ["e0.0"])
+    iota(T.e0[:, 1:32:4], [[0, 2], [8, 2], [0, 2]], -4, 0, ["e0.1"])
+    iota(T.e0[:, 2:32:4], [[4, 2], [0, 4]], -2, 0, ["e0.2"])
+    iota(T.e0[:, 3:32:4], [[0, 8]], -1, 0, ["e0.3"])
     iota(T.ji[:, :], [[16, 32]], 320, 1, ["ji"])
-    act(T.ma2[:, :], T.ma1[:, :], ["ma1"], ["ma2"], scale=2.0)
+    act(T.m4[:, 2:3], T.bo[:, 3:4], ["bo3"], ["m2"])
+    act(T.m4[:, 1:2], T.bo[:, 2:3], ["bo2", "bo3"], ["m1"], F.Sign, bias=T.bo[:, 3:4])
+    act(T.ini[:, :], T.fl0[:, :], ["fl0"], ["ini"], scale=-256.0)
+    act(T.m4[:, 0:1], T.bo[:, 1:2], ["bo1", "m1"], ["m0"], F.Sign, bias=T.m4[:, 1:2])
+    act(T.subl[:, :], T.lf[:, :], ["lf"], ["subl"], F.Identity, bias=15360.0, scale=-1024.0)
+    act(T.ad[:, :], T.nd[:, :], ["nd"], ["ad"], F.Abs, bias=0.5, scale=-1.0)
+    act(T.ma2[:, 0:240], T.ma1[:, 0:240], ["ma1"], ["ma2"], scale=2.0)
     act(T.d0l[:, :], T.ma1[:, :], ["ma1"], ["d0l"], F.Identity, bias=1024.0, scale=-66560.0)
     act(T.d0t[:, :], T.i8[:, :], ["i8"], ["d0t"], F.Sign)
     for b in range(4):
@@ -193,30 +236,26 @@ def rank_program(g, core, T, topo):
     vts(T.ofl[:, 0:1], T.sei[:, 0:1], T.tr[:, 0:1], None, A.add, None, ["sei", "tr"], ["ofl0"])
     vcp(T.ofl[:, 1:20], T.sei[:, 1:20], ["sei"], ["ofl"])
     vcp(T.dd[:, 0:656].indirect(T.ofl[:, 0:20]), T.i512[:, 0:C], ["ofl", "ofl0", "i512"], ["dd", "dd1"])
-    later(vcp, T.ull[:, :], T.uli[:, :], ["uli"], ["ull"])
+    later(vcp, T.ull[:, :], T.i512[:, 0:128:16], ["i512"], ["ull"])
     later(vts, T.ai[:, :], T.sei[:, :], 1, None, A.arith_shift_right, None, ["sei"], ["ai"])
-    later(vset, T.t4[:, :], 0, ["t4%d" % j for j in range(4)])
+    later(vts, T.sg[:, :], T.nd[:, :], 0.0, 0.5, A.is_le, A.subtract, ["nd"], ["sg"])
     later(vcp, T.parl[:, :], T.ai[:, :], ["ai"], ["parl"])
-    for j in range(3):
-        later(vts, T.t4[:, j:j + 1], T.li[:, :], 7 >> j, None, A.bitwise_and, None, ["li"], ["t4%d" % j])
-    for j in range(4):
-        later(vts, T.w4[:, j:j + 1], T.x4[:, j:j + 1], 32.0, float(-(128 >> j)), A.mult, A.add, ["x4%d" % j], ["w4%d" % j])
-    later(vts, T.m8[:, :], T.t4[:, :], 0.0, None, A.not_equal, None, ["t4%d" % j for j in range(4)], ["m8"])
-    for j in range(4):
-        later(vts, T.e0[:, 16 + j:80:8], T.z8[:, :], T.w4[:, j:j + 1], None, A.add, None, ["z8", "w4%d" % j], ["e0.%d" % j])
-    later(vtt, T.e0[:, 0:4], T.w4[:, :], T.m8[:, 0:4], A.mult, ["w40", "w41", "w42", "w43", "m8"], ["e0.8"])
-    later(vtt, T.oh[:, 0:3], T.m8[:, 0:3], T.m8[:, 1:4], A.subtract, ["m8"], ["oh"])
-    later(vts, T.fl0[:, :], T.lf[:, :], 0.0, None, A.is_equal, None, ["lf"], ["fl0"])
-    later(vset, T.d0t[:, 0:1], 1.0, ["d0t"])
-    later(vts, T.subl[:, :], T.lf[:, :], -1024.0, 15360.0, A.mult, A.add, ["lf"], ["subl"])
-    later(vts, T.ini[:, :], T.fl0[:, :], -256.0, None, A.mult, None, ["fl0"], ["ini"])
+    later(vtt, T.an[:, :], T.ad[:, :], T.zz[:, :], A.is_lt, ["ad"] + ZZ, ["an"])
+    later(vtt, T.oh[:, 0:3], T.m4[:, 0:3], T.m4[:, 1:4], A.subtract, ["m0", "m1", "m2", "m3"], ["oh"])
+    later(vtt, T.w1[:, :], T.sg[:, :], T.zz[:, :], A.mult, ["sg"] + ZZ, ["w1"])
+    later(vset, T.an[:, 0:1], 0.0, ["an"])
+    later(vtt, T.zl[:, :], T.zz[:, :], T.ma1[:, 0:16], A.mult, ZZ + ["ma1"], ["zl"])
+    later(vtt, T.w2[:, :], T.w1[:, :], T.an[:, :], A.mult, ["w1", "an"], ["w2"])
+    later(vred, T.zr[:, :], T.zl[:, :], ["zl"], ["zr"])
+    later(act, T.wt0[:, :], T.w2[:, :], ["w2"], ["wt0"], scale=32.0)
+    later(vts, T.tm[:, :], T.zz[:, :], T.zr[:, 0:1], None, A.is_gt, None, ZZ + ["zr"], ["tm"])
+    later(vtt, T.fm[:, :], T.fc[:, :], T.ma1[:, 0:64], A.mult, FC + ["ma1"], ["fm"])
     later(vtt, T.yo[:, 0:3], T.yt[:, 1:4], T.oh[:, 0:3], A.mult, ["oh", "yt1", "yt2", "yt3"], ["yo"])
-    later(vcp, T.ls[:, 32:36], T.yt[:, 0:4], ["yt0", "yt1", "yt2", "yt3"], ["lst"])
+    later(vscan, T.fs[:, :], T.d0r[:, 0:64], T.fm[:, :], 0.0, A.mult, A.add, ["fm", "d0r"], ["fs"])
     later(vred, T.yo[:, 4:5], T.yo[:, 0:3], ["yo"], ["yo4"])
-    later(vtt, T.fm[:, :], T.fc[:, :], T.ma1[:, 0:128], A.mult, ["fc%d" % j for j in range(14)] + ["ma1"], ["fm"])
+    later(vcp, T.tl[:, 0:4], T.fs[:, 15:64:16], ["fs"], ["tl"])
     later(vcp, T.ls[:, 31:32], T.yo[:, 4:5], ["yo4"], ["ls31"])
-    later(vscan, T.fs[:, :], T.d0r[:, 0:128], T.fm[:, :], 0.0, A.mult, A.add, ["fm", "d0r"], ["fs"])
-    later(vcp, T.tl[:, 0:8], T.fs[:, 15:128:16], ["fs"], ["tl"])
+    later(vtt, T.wm0[:, :], T.wt0[:, :], T.tm[:, :], A.mult, ["wt0", "tm"], ["wm0"])
 
     for j in range(4):
         vtt(T.g16[:, 16 * j:16 * j + 16], T.dd[:, 0:640].indirect(T.wo[:, 2 * j:2 * j + 1]), T.ma1[:, 0:16], A.mult,
@@ -244,7 +283,7 @@ def rank_program(g, core, T, topo):
             vcp(T.ur[:, 0:128].bitcast(dt.uint32), T.uq[:, 0:128].bitcast(dt.uint32).indirect(T.ull[:, 0:8]), ["uq", "ull"], ["ur"])
             act(T.urs[:, 0:128], T.us[:, 0:128].indirect(T.ull[:, 0:8]), ["uq", "ull"], ["urs"])
         elif n == 2:
-            quant(T.q0[:, 0:C], T.qs0[:, 0:C], T.x0[:, 0:1280], ["x0"], ["q0"])
+            quant(T.q0[:, 0:C], T.qs0[:, 0:C], T.x0[:, 0:1280], ["x0"], ["q0.0"])
         else: fill()
         y = T.gs[:, h + 15:h + k:16]
         if n < 8:
@@ -255,62 +294,100 @@ def rank_program(g, core, T, topo):
     fill(len(spare))
 
     def labels(k):
-        send(T.ll[:, 32 * k:32 * k + 32], T.ls[:, 0:32], "lb%d" % k, partner[k], LS)
+        send(T.ll[:, 32 * k:32 * k + 32], T.ls[:, 0:32], "lb%d" % k, relay[k] or partner[k], LS)
 
     labels(0)
 
     later(vcp, T.yf[:, :], T.ls[:, :], LS, ["yf"])
-    later(vts, T.tls[:, 0:5], T.fs[:, 15:80:16], 0.0625, 15.0625, A.mult, A.add, ["fs"], ["tls"])
-    later(vtt, T.y32[:, :], T.yf[:, 0:32], T.ji[:, :], A.subtract, ["yf", "ji"], ["y32"])
-    later(vcp, T.lab[:, :], T.yf[:, 0:36].indirect(T.tls[:, 0:5]), ["yf", "tls"], ["lab"])
-    later(vtt, T.eqv[:, 0:79], T.lab[:, 1:80], T.lab[:, 0:79], A.is_equal, ["lab"], ["eqv"])
-    later(vtt, T.eqr[:, :], T.lab[:, 23:80:8], T.yf[:, 8:16], A.is_equal, ["lab", "yf"], ["eqr"])
-    later(vtt, T.eqv[:, 23:80:8], T.lab[:, 23:80:8], T.yf[:, 0:8], A.is_equal, ["lab", "yf"], ["eqv"])
-    later(vtt, T.eqv[:, 0:8], T.eqv[:, 0:8], T.m8[:, :], A.mult, ["eqv", "m8"], ["eqv"])
-    later(vscan, T.cs[:, 0:80], T.d0t[:, :], T.eqv[:, :], T.fl0[:, 0:1], A.mult, A.add, ["eqv", "d0t", "fl0"], ["cs"])
-    later(vtt, T.cs[:, 80:88], T.cs[:, 22:80:8], T.eqr[:, :], A.add, ["cs", "eqr"], ["csr"])
-    later(vts, T.z32[:, :], T.cs[:, 0:88].indirect(T.tl[:, 6:8]), 0.0, None, A.is_equal, None, ["cs", "csr", "tl"], ["z32"])
+    later(vts, T.tls[:, 0:2], T.fs[:, 15:32:16], 0.0625, 15.0625, A.mult, A.add, ["fs"], ["tls"])
+    later(vtt, T.eqp[:, :], T.yt[:, 0:4], T.yt[:, 1:5], A.is_equal, ["yt0", "yt1", "yt2", "yt3", "yt4"], ["eqp"])
+    later(vtt, T.y32[:, :], T.yf[:, :], T.ji[:, :], A.subtract, ["yf", "ji"], ["y32"])
+    later(vcp, T.lab[:, :], T.yf[:, :].indirect(T.tls[:, 0:2]), ["yf", "tls"], ["lab"])
+    later(vtt, T.eqm[:, :], T.eqp[:, :], T.m4[:, :], A.mult, ["eqp", "m0", "m1", "m2", "m3"], ["eqm"])
+    later(vred, T.cb[:, :], T.eqp[:, :], ["eqp"], ["cb"])
+    later(vtt, T.eqv[:, 0:31], T.lab[:, 1:32], T.lab[:, 0:31], A.is_equal, ["lab"], ["eqv"])
+    later(vred, T.ct[:, :], T.eqm[:, :], ["eqm"], ["ct"])
+    later(vtt, T.eqr[:, :], T.lab[:, 3:32:4], T.yf[:, 8:16], A.is_equal, ["lab", "yf"], ["eqr"])
+    later(vtt, T.eqv[:, 3:32:4], T.lab[:, 3:32:4], T.yf[:, 0:8], A.is_equal, ["lab", "yf"], ["eqv"])
+    later(vts, T.cs[:, 41:42], T.ct[:, :], T.cb[:, 0:1], T.fl0[:, 0:1], A.subtract, A.add, ["ct", "cb", "fl0"], ["cst"])
+    later(vscan, T.cs[:, 0:32], T.d0t[:, :], T.eqv[:, :], 0.0, A.mult, A.add, ["eqv", "d0t"], ["cs"])
+    later(vtt, T.cs[:, 32:40], T.cs[:, 2:32:4], T.eqr[:, :], A.add, ["cs", "eqr"], ["csr"])
+    later(vts, T.z32[:, :], T.cs[:, 0:42].indirect(T.tl[:, 2:4]), T.cb[:, 0:1], 0.0, A.add, A.is_equal, ["cs", "csr", "cst", "cs0", "cb", "tl"], ["z32"])
     later(vtt, T.zy[:, :], T.z32[:, :], T.y32[:, :], A.mult, ["z32", "y32"], ["zy"])
     later(vtt, T.o32[:, :], T.zy[:, :], T.ji[:, :], A.add, ["zy", "ji"], ["o32"])
     later(vcp, T.ol[:, :], T.o32[:, :], ["o32"], ["ol"])
 
     for r in range(3):
-        q, qs, qt = T["q%d" % r], T["qs%d" % r], "q%d" % r
+        q, qs, qt = T["q%d" % (r % 2)], T["qs%d" % (r % 2)], "q%d" % (r % 2)
         Q, QS = q[:, 0:C], qs[:, 0:C]
-        mm(0, T.ur[:, 0:128], T.urs[:, 0:128], Q, QS, [qt, "ur", "urs"])
-        for b in range(4):
-            mm(1 + b, T.wq[:, 128 * b:128 * b + 128], T.wqs[:, 128 * b:128 * b + 128], Q, QS, [qt, "wq", "wqs"])
-        vts(T.tb[:, :], bank(0), 0.0, 0.5, A.is_ge, A.subtract, ["bank0"], ["tb"])
+        parts = PARTS if r else [(0, C)]
+        qp = ["%s.%d" % (qt, i) for i in range(len(parts))]
+        wb, fb, ab = [[1, 2, 3, 4], [6, 7, 0, 5]], [[6, 7, 0, 5], [1, 2, 3, 4]][len(parts) - 1], [[1, 2, 3, 4], [6, 7, 0, 5]][len(parts) - 1]
+        far = relay[r] is not None
+        hq, hs, lq, lqs = T["hq%d" % r], T["hs%d" % r], T["lq%d" % r], T["lqs%d" % r]
+
+        def scores(i):
+            c0, c1 = parts[i]
+            mm(5 * i, T.ur[:, 0:128], T.urs[:, 0:128], q[:, c0:c1], qs[:, c0:c1], [qp[i], "ur", "urs"], c1 - c0)
+
+        def layer(i):
+            c0, c1 = parts[i]
+            for b in range(4):
+                mm(wb[i][b], T.wq[:, 128 * b:128 * b + 128], T.wqs[:, 128 * b:128 * b + 128], q[:, c0:c1], qs[:, c0:c1], [qp[i], "wq", "wqs"], c1 - c0)
+            for b in range(4):
+                k = wb[i][b]
+                act(T.hb[:, 4 * c0 + b:4 * c1:4], T.ps[:, 512 * k:512 * k + c1 - c0], ["bank%d" % k], ["hb%d.%d" % (i, b)], scale=0.03125)
+
+        def pack(c0, c1, ii, t):
+            quant(hq[:, c0:c1], hs[:, c0:c1], T.hb[:, 4 * c0:4 * c1], ["hb%d.%d" % (i, b) for i in ii for b in range(4)], [t])
+
+        def signs(i):
+            c0, c1 = parts[i]
+            vts(T.tb[:, c0:c1], T.ps[:, 2560 * i:2560 * i + c1 - c0], 0.0, 0.5, A.is_ge, A.subtract, ["bank%d" % (5 * i)], ["tb%d" % i])
+
+        if far:
+            c0, c1 = parts[0]
+            layer(0)
+            scores(0)
+            scores(1)
+            pack(c0, c1, [0], "hqa")
+            send(hq[:, c0:c1].bitcast(dt.uint8), hq[:, c0:c1].bitcast(dt.uint8), "hand", relay[r], ["hqa"])
+            send(lqs[:, c0:c1], hs[:, c0:c1], "sra", partner[r], ["hqa"])
+        else:
+            scores(0)
+            layer(0)
+            if r: scores(1)
+        for i in range(len(parts)): signs(i)
+        if r: layer(1)
         fill()
-        vtt(T.mg[:, :], T.tb[:, 0:C].indirect(T.ls[:, 16:36]), T.ma2[:, :], A.mult, ["tb", "ma2"] + LS, ["mg"])
+        vtt(T.mg[:, :], T.tb[:, 0:C].indirect(T.ls[:, 16:32]), T.ma2[:, 0:256], A.mult, ["tb0", "tb1", "ma2", "ma2b"] + LS, ["mg"])
         fill()
-        vscan(T.sc[:, :], T.d0r[:, :], T.mg[:, :], 0.0, A.mult, A.add, ["mg", "d0r"], ["sc"])
-        fill()
+        vscan(T.sc[:, :], T.d0r[:, 0:240], T.mg[:, 0:240], 0.0, A.mult, A.add, ["mg", "d0r"], ["sc"])
+        o, n = r % 2, 1 - r % 2
+        vtt(T["wt%d" % n][:, :], T.mg[:, 240:256], T["wt%d" % o][:, :], A.mult, ["mg", "wt%d" % o], ["wt%d" % n])
         eo, en, te, tn = (T.e0, T.e1, E0, ["e1"]) if r % 2 == 0 else (T.e1, T.e0, ["e1"], E0)
-        vtt(en[:, :], T.sc[:, 0:C].indirect(T.tl[:, 0:5]), eo[:, :], A.mult, ["sc", "tl"] + te, tn)
-        fill()
-        vscan(T.pp[:, 0:80], T.d0t[:, :], en[:, :], T.ini[:, 0:1], A.mult, A.add, tn + ["d0t", "ini"], ["pp"])
-        fill()
-        vtt(T.pp[:, 80:88], T.pp[:, 22:80:8], en[:, 23:80:8], A.subtract, ["pp"] + tn, ["ppr"])
-        fill()
+        vtt(en[:, :], T.sc[:, 0:240].indirect(T.tl[:, 0:2]), eo[:, :], A.mult, ["sc", "tl"] + te, tn)
+        vtt(T["wm%d" % n][:, :], T.mg[:, 240:256], T["wm%d" % o][:, :], A.mult, ["mg", "wm%d" % o], ["wm%d" % n])
+        vred(T.ba[:, :], T["wt%d" % n][:, :], ["wt%d" % n], ["ba"])
+        vscan(T.pp[:, 0:32], T.d0t[:, :], en[:, :], 0.0, A.mult, A.add, tn + ["d0t"], ["pp"])
+        vred(T.bt[:, :], T["wm%d" % n][:, :], ["wm%d" % n], ["bt"])
+        vtt(T.pp[:, 32:40], T.pp[:, 2:32:4], en[:, 3:32:4], A.subtract, ["pp"] + tn, ["ppr"])
+        vts(T.pp[:, 41:42], T.bt[:, :], T.ba[:, 0:1], T.ini[:, 0:1], A.subtract, A.add, ["bt", "ba", "ini"], ["ppt"])
         pl, pa = T.pl[:, 32 * r:32 * r + 32], T.pa[:, 32 * r:32 * r + 32]
-        vts(pl, T.pp[:, 0:88].indirect(T.tl[:, 6:8]), 256.0, None, A.add, None, ["pp", "ppr", "tl"], ["pl%d" % r])
+        vts(pl, T.pp[:, 0:42].indirect(T.tl[:, 2:4]), T.ba[:, 0:1], 256.0, A.add, A.add, ["pp", "ppr", "ppt", "pp0", "ba", "tl"], ["pl%d" % r])
         send(pa, pl, "pr%d" % r, partner[r], ["pl%d" % r])
         fill()
-        hb = T["hb%d" % r]
-        for b in range(4):
-            act(hb[:, b:1280:4], bank(1 + b), ["bank%d" % (1 + b)], ["hb%d.%d" % (r, b)], scale=0.03125)
-        quant(T["hq%d" % r][:, 0:C], T["hs%d" % r][:, 0:C], hb[:, 0:1280], ["hb%d.%d" % (r, b) for b in range(4)], ["hq%d" % r])
-        send(T["lq%d" % r][:, 0:C].bitcast(dt.uint8), T["hq%d" % r][:, 0:C].bitcast(dt.uint8), "cr%d" % r, partner[r], ["hq%d" % r])
-        send(T["lqs%d" % r][:, 0:C], T["hs%d" % r][:, 0:C], "sr%d" % r, partner[r], ["hq%d" % r])
+        c0, c1 = parts[1] if far else (0, C)
+        pack(c0, c1, [1] if far else range(len(parts)), "hq%d" % r)
+        send(lq[:, c0:c1].bitcast(dt.uint8), hq[:, c0:c1].bitcast(dt.uint8), "cr%d" % r, partner[r], ["hq%d" % r])
+        send(lqs[:, c0:c1], hs[:, c0:c1], "sr%d" % r, partner[r], ["hq%d" % r])
         fill()
         if r == 0:
             labels(1)
             labels(2)
             quant(T.eq[:, :], T.es[:, :], T.eb[:, :], ["eb0", "eb1", "eb2", "eb3"], ["eq"])
-        fb = [5, 6, 7, 0]
         for b in range(4):
-            mm(fb[b], T.eq[:, 128 * b:128 * b + 128], T.es[:, 128 * b:128 * b + 128], Q, QS, [qt, "eq"])
+            mm(fb[b], T.eq[:, 128 * b:128 * b + 128], T.es[:, 128 * b:128 * b + 128], Q, QS, qp + ["eq"])
         act(T.prep[:, :], T.i512[:, :].indirect(pl), ["i512", "i512b", "pl%d" % r], ["prep"])
         if r == 0:
             for b in range(4):
@@ -321,14 +398,16 @@ def rank_program(g, core, T, topo):
             vts(T.al[:, :], T.als[:, 15:C:16], T.subl[:, 0:1], None, A.subtract, None, ["als", "subl"], ["al"])
             lastw["ll0"] = ("lb0", len(topo.engines(core, partner[0])))
             act(T.lr[:, 0:512], T.i512[:, 0:C].indirect(T.ll[:, 0:32]), ["i512", "ll0"], ["lr0"])
-            for b in range(4):
+            for b in range(2):
                 act(T.fg[:, C * b:C * b + C], T.fw[:, C * b:C * b + C].indirect(T.parl[:, 0:20]), ["fw%d" % b, "parl"], ["fg%d" % b])
         act(T.brep[:, :], T.prep[:, :].indirect(T.al[:, 0:20]), ["prep", "al"], ["brep"])
         if r:
             for b in range(4):
                 vcp(T.fw[:, C * b:C * b + C], bank(fb[b]), ["bank%d" % fb[b]], ["fw%d" % b])
-            for b in range(4):
-                act(T.fg[:, C * b:C * b + C], T.fw[:, C * b:C * b + C].indirect(T.parl[:, 0:20]), ["fw%d" % b, "parl"], ["fg%d" % b])
+        if r == 1:
+            quant(T.vq[:, :], T.vs[:, :], T.vb[:, :], ["vb"], ["vq"])
+        for b in range(0 if r else 2, 4):
+            act(T.fg[:, C * b:C * b + C], T.fw[:, C * b:C * b + C].indirect(T.parl[:, 0:20]), ["fw%d" % b, "parl"], ["fg%d" % b])
         k = len(topo.engines(core, partner[r]))
         lastw["pa%d" % r], lastw["lq%d" % r], lastw["lqs%d" % r] = ("pr%d" % r, k), ("cr%d" % r, k), ("sr%d" % r, k)
         zt = (T.zt[:, :].indirect(pa), T.lr[:, 512 * r:512 * r + 512], ["pa%d" % r, "lr%d" % r], ["zt"])
@@ -341,27 +420,34 @@ def rank_program(g, core, T, topo):
         vts(T.ml[:, :], T.msc[:, 15:C:16], T.subl[:, 0:1], None, A.subtract, None, ["msc", "subl"], ["ml"])
         if r == 2:
             store("Y", T.im[:, :], T.mr[0:128:16, :], ["mr"])
-        for b in range(4):
-            mm(1 + b, T.eq[:, 128 * b:128 * b + 128], T.es[:, 128 * b:128 * b + 128], T["lq%d" % r][:, 0:C], T["lqs%d" % r][:, 0:C], ["lq%d" % r, "lqs%d" % r, "eq"])
-        for b in range(4):
-            act(T.aw[:, C * b:C * b + C], bank(1 + b), ["bank%d" % (1 + b)], ["aw%d" % b])
-        xr = T["xr%d" % r]
-        for b in range(4):
-            vtt(xr[:, b:1280:4], T.aw[:, C * b:C * b + C].indirect(T.ml[:, 0:20]), T.fg[:, C * b:C * b + C], A.add, ["aw%d" % b, "ml", "fg%d" % b], ["xr%d.%d" % (r, b)])
+        runs = [(0, C, ab, ["lq%d" % r, "lqs%d" % r])]
+        if far:
+            lastw["lqa"], lastw["lqsa"] = ("handed", len(topo.engines(theirs[r], core))), ("sra", k)
+            runs = [parts[0] + ([1, 2, 3, 4], ["lqa", "lqsa"]), parts[1] + (ab, ["lq%d" % r, "lqs%d" % r])]
+        for c0, c1, bb, tt in runs:
+            for b in range(4):
+                mm(bb[b], T.eq[:, 128 * b:128 * b + 128], T.es[:, 128 * b:128 * b + 128], lq[:, c0:c1], lqs[:, c0:c1], tt + ["eq"], c1 - c0)
+        for j, (c0, c1, bb, tt) in enumerate(runs):
+            for b in range(4):
+                act(T.aw[:, C * b + c0:C * b + c1], T.ps[:, 512 * bb[b]:512 * bb[b] + c1 - c0], ["bank%d" % bb[b]], ["aw%d.%d" % (j, b)])
         n = r + 1
-        quant(T["q%d" % n][:, 0:C], T["qs%d" % n][:, 0:C], xr[:, 0:1280], ["xr%d.%d" % (r, b) for b in range(4)], ["q%d" % n])
+        for i, (c0, c1) in enumerate(PARTS):
+            for b in range(4):
+                vtt(T.xr[:, 4 * c0 + b:4 * c1:4], T.aw[:, C * b:C * b + C].indirect(T.ml[:, c0 // 16:c1 // 16]), T.fg[:, C * b + c0:C * b + c1], A.add,
+                    ["aw0.%d" % b, "aw1.%d" % b, "ml", "fg%d" % b], ["xr%d.%d" % (i, b)])
+            quant(T["q%d" % (n % 2)][:, c0:c1], T["qs%d" % (n % 2)][:, c0:c1], T.xr[:, 4 * c0:4 * c1], ["xr%d.%d" % (i, b) for b in range(4)], ["q%d.%d" % (n % 2, i)])
         if r < 2:
-            lastw["ll%d" % n] = ("lb%d" % n, len(topo.engines(core, partner[n])))
+            lastw["ll%d" % n] = ("lb%d" % n, len(topo.engines(theirs[n] or partner[n], core)))
             act(T.lr[:, 512 * n:512 * n + 512], T.i512[:, 0:C].indirect(T.ll[:, 32 * n:32 * n + 32]), ["i512", "ll%d" % n], ["lr%d" % n])
-        if r == 0:
-            quant(T.vq[:, :], T.vs[:, :], T.vb[:, :], ["vb"], ["vq"])
 
-    mm(5, T.vq[:, 0:128], T.vs[:, 0:128], T.q3[:, 0:C], T.qs3[:, 0:C], ["q3", "vq"])
-    store("Y", T.oc[:, :], T.q3[:, 0:C].bitcast(dt.uint8), ["q3"])
-    for k in range(4):
-        store("S" if k % 2 else "Y", T.osc[4 * k:4 * k + 4, :], T.qs3[32 * k:32 * k + 4, 0:C], ["q3"])
-    vcp(T.ysb[:, :], bank(5), ["bank5"], ["ysb"])
-    store("Y", T.y[:, :], T.ysb[:, :], ["ysb"])
+    for i, (c0, c1) in enumerate(PARTS):
+        t = "q1.%d" % i
+        mm(5 * i, T.vq[:, 0:128], T.vs[:, 0:128], T.q1[:, c0:c1], T.qs1[:, c0:c1], [t, "vq"], c1 - c0)
+        vcp(T.ysb[:, c0:c1], T.ps[:, 2560 * i:2560 * i + c1 - c0], ["bank%d" % (5 * i)], ["ysb%d" % i])
+        store("Y", T.oc[:, 4 * c0:4 * c1], T.q1[:, c0:c1].bitcast(dt.uint8), [t])
+        for k in range(4):
+            store("S", T.osc[4 * k:4 * k + 4, c0:c1], T.qs1[32 * k:32 * k + 4, c0:c1], [t])
+        store("Y", T.y[:, c0:c1], T.ysb[:, c0:c1], ["ysb%d" % i])
     for k in ("V", "S", "T", "G"):
         wait("G", ("c" + k, cnt[k]))
     g.wait_ge(T.sem.stored, stores[0])

import numpy as np
from concourse.mybir import dt, AluOpType, AxisListType, ActivationFunctionType

C = 320
STEP = [1, 2, 4]
PARTS = [(0, 192), (192, 320)]
A = AluOpType
F = ActivationFunctionType

SCRATCH = {"ps": ("psum", [128, 4096], "float32")}
for _n, _w, _d in (
        ("x0", 1280, "bfloat16"), ("ub", 512, "bfloat16"), ("vb", 512, "bfloat16"), ("sei", 20, "int32"),
        ("uq", 128, "float8_e4m3fn_x4"), ("us", 128, "uint8"), ("ur", 128, "float8_e4m3fn_x4"), ("urs", 128, "uint8"),
        ("vq", 128, "float8_e4m3fn_x4"), ("vs", 128, "uint8"), ("wq", 512, "float8_e4m3fn_x4"), ("wqs", 512, "uint8"),
        ("idt", 128, "bfloat16"), ("eb", 2048, "bfloat16"), ("eq", 512, "float8_e4m3fn_x4"), ("es", 512, "uint8"),
        ("pi", 1, "int32"), ("li", 1, "int32"), ("lf", 1, "float32"), ("i16", 320, "float32"), ("i512", 512, "float32"),
        ("ma1", 320, "bfloat16"), ("ma2", 320, "bfloat16"), ("d0r", 320, "bfloat16"), ("d0l", 320, "float32"),
        ("subl", 1, "float32"), ("i8", 32, "float32"), ("d0t", 32, "float32"), ("x4", 4, "int32"), ("bo", 4, "float32"),
        ("m4", 4, "float32"), ("oh", 4, "float32"), ("fl0", 1, "float32"), ("ini", 1, "float32"), ("tr", 1, "float32"),
        ("zz", 16, "float32"), ("nd", 16, "float32"), ("ad", 16, "float32"), ("sg", 16, "float32"), ("an", 16, "float32"),
        ("w1", 16, "float32"), ("w2", 16, "float32"), ("zl", 16, "float32"), ("zr", 1, "float32"), ("tm", 16, "float32"),
        ("wt0", 16, "float32"), ("wt1", 16, "float32"), ("wm0", 16, "float32"), ("wm1", 16, "float32"), ("ba", 1, "float32"), ("bt", 1, "float32"),
        ("ji", 32, "float32"), ("fc", 64, "float32"), ("fm", 64, "float32"), ("fs", 64, "float32"), ("tl", 4, "uint16"), ("tls", 2, "uint16"),
        ("ull", 8, "uint16"),
        ("ai", 20, "int32"), ("ofl", 20, "uint16"), ("parl", 20, "uint16"), ("dd", 656, "float32"), ("wo", 8, "uint16"), ("wv", 32, "uint16"),
        ("g16", 64, "float32"), ("yt", 8, "float32"), ("yo", 8, "float32"), ("gg", 512, "float32"), ("gs", 512, "float32"),
        ("ls", 32, "uint16"), ("yf", 32, "float32"), ("lab", 32, "float32"), ("eqv", 32, "float32"), ("eqr", 8, "float32"),
        ("eqp", 4, "float32"), ("eqm", 4, "float32"), ("cb", 1, "float32"), ("ct", 1, "float32"), ("cs", 42, "float32"), ("z32", 32, "float32"), ("y32", 32, "float32"), ("zy", 32, "float32"), ("o32", 32, "float32"), ("ol", 32, "uint16"),
        ("at", 960, "float32"), ("als", 320, "float32"), ("al", 20, "uint16"),
        ("tb", 320, "bfloat16"), ("mg", 256, "bfloat16"), ("sc", 240, "bfloat16"), ("e0", 32, "float32"), ("e1", 32, "float32"),
        ("pp", 42, "float32"), ("prep", 512, "float32"), ("brep", 320, "float32"), ("bsc", 320, "float32"), ("bl", 20, "uint16"),
        ("zt", 512, "float32"), ("msc", 320, "float32"), ("ml", 20, "uint16"), ("mr", 320, "float32"), ("ysb", 320, "float32"),
        ("fw", 1280, "bfloat16"), ("fg", 1280, "bfloat16"), ("aw", 1280, "bfloat16"),
        ("pl", 96, "uint16"), ("pa", 96, "uint16"), ("ll", 96, "uint16"), ("lr", 1536, "float32")):
    SCRATCH[_n] = ("sbuf", [128, _w], _d)
for _r in range(2):
    SCRATCH["q%d" % _r] = ("sbuf", [128, 320], "float8_e4m3fn_x4")
    SCRATCH["qs%d" % _r] = ("sbuf", [128, 320], "uint8")
SCRATCH["xr"] = SCRATCH["hb"] = ("sbuf", [128, 1280], "bfloat16")
for _r in range(3):
    SCRATCH["hq%d" % _r] = ("sbuf", [128, 320], "float8_e4m3fn_x4")
    SCRATCH["hs%d" % _r] = ("sbuf", [128, 320], "uint8")
    SCRATCH["lq%d" % _r] = ("sbuf", [128, 320], "float8_e4m3fn_x4")
    SCRATCH["lqs%d" % _r] = ("sbuf", [128, 320], "uint8")

SEMAPHORES = ["cV", "cS", "cT", "cG", "sent", "stored", "hand", "handed", "sra", "lse", "lx", "lu", "lv", "lwc", "lws"]
for _r in range(3):
    SEMAPHORES += ["pr%d" % _r, "lb%d" % _r, "cr%d" % _r, "sr%d" % _r]


def relay_of(T, topo, rank, s):
    core, dst = T.cores[rank], T.cores[rank ^ s]
    if topo.chip(core) == topo.chip(dst): return None
    mine = [c for c in topo.cores_of(core) if T.rank_of(c) is not None]
    free = [c for c in topo.cores_of(core) if T.rank_of(c) is None and topo.die(c) != topo.die(core) and topo.may_write(c, dst)]
    return free[mine.index(core) % len(free)]


def hand_on(g, core, T, topo):
    for rank in range(len(T.cores)):
        for k, s in enumerate(STEP):
            if relay_of(T, topo, rank, s) != core: continue
            src, dst = T.cores[rank], T.cores[rank ^ s]
            rid, pid, _s = topo.addr(dst)
            m, n, got = topo.mask(core, dst), len(topo.engines(core, dst)), len(topo.engines(src, core))
            c0, c1 = PARTS[0]
            ll, hq, lq = T.ll[:, 32 * k:32 * k + 32], T["hq%d" % k][:, c0:c1].bitcast(dt.uint8), T["lq%d" % k][:, c0:c1].bitcast(dt.uint8)
            g.wait_ge(T.sem["lb%d" % k], got)
            g.remote_dma(ll, ll, T.sem["lb%d" % k], T.sem.sent, pid, rid, m)
            g.wait_ge(T.sem.hand, got)
            g.remote_dma(lq, hq, T.sem.handed, T.sem.sent, pid, rid, m)
            g.wait_ge(T.sem.sent, 2 * n)


def rank_program(g, core, T, topo):
    rank = T.rank_of(core)
    if rank is None:
        hand_on(g, core, T, topo)
        return
    eng = {"V": g.vector, "S": g.scalar, "T": g.tensor, "G": g, "Y": g.sync}
    cnt = {"V": 0, "S": 0, "T": 0, "G": 0}
    known = {q: {} for q in eng}
    lastw, readers = {}, {}

    def wait(q, stamp):
        sem, val = stamp
        if known[q].get(sem, 0) < val:
            eng[q].wait_ge(T.sem[sem], val)
            known[q][sem] = val

    def order(q, r, w):
        need = {}
        for t in r:
            if t in lastw: need[lastw[t][0]] = max(need.get(lastw[t][0], 0), lastw[t][1])
        for t in w:
            if t in lastw: need[lastw[t][0]] = max(need.get(lastw[t][0], 0), lastw[t][1])
            for s, v in readers.get(t, []): need[s] = max(need.get(s, 0), v)
        for s in sorted(need): wait(q, (s, need[s]))

    def mark(r, w, stamp):
        for t in r: readers.setdefault(t, []).append(stamp)
        for t in w:
            lastw[t] = stamp
            readers[t] = []

    def op(q, call, r, w):
        bank = [t for t in r if t.startswith("bank")]
        r, w = [t for t in r if t not in bank], list(w) + bank
        order(q, r, w)
        cnt[q] += 1
        call(eng[q]).then_inc(T.sem["c" + q], 1)
        mark(r, w, ("c" + q, cnt[q]))

    def load(q, out, in_, w, sem):
        eng[q].dma_start(out, in_).then_inc(T.sem[sem], 16)
        mark([], [w], (sem, 16))

    stores = [0]

    def store(q, out, in_, r):
        order(q, r, [])
        eng[q].dma_start(out, in_).then_inc(T.sem.stored, 16)
        stores[0] += 16

    def vts(out, in0, s1, s2, op0, op1, r, w):
        if op1 is None: op("V", lambda e: e.tensor_scalar(out, in0, s1, s2, op0), r, w)
        else: op("V", lambda e: e.tensor_scalar(out, in0, s1, s2, op0, op1), r, w)

    def vtt(out, a, b, o, r, w): op("V", lambda e: e.tensor_tensor(out, a, b, o), r, w)
    def vcp(out, in_, r, w): op("V", lambda e: e.tensor_copy(out, in_), r, w)
    def vset(ap, c, w): op("V", lambda e: e.memset(ap, c), [], w)
    def vred(out, in_, r, w): op("V", lambda e: e.tensor_reduce(out, in_, AxisListType.X, A.add), r, w)
    def vscan(out, d0, d1, ini, o0, o1, r, w): op("V", lambda e: e.tensor_tensor_scan(out, d0, d1, ini, o0, o1), r, w)
    def iota(ap, pat, base, cm, w): op("G", lambda e: e.iota(ap, pat, base, cm, allow_small_or_imprecise_dtypes=True), [], w)
    def act(out, in_, r, w, f=F.Copy, **k): op("S", lambda e: e.activation(out, in_, f, **k), r, w)
    def quant(c, s, t, r, w): op("V", lambda e: e.quantize_mx(c, s, t), r, w)

    def mm(bank, lc, lsc, rc, rsc, r, n=C):
        out = T.ps[:, 512 * bank:512 * bank + n]
        op("T", lambda e: e.matmul_mx(out, lc, lsc, rc, rsc, True, True), r, ["bank%d" % bank])

    def bank(b): return T.ps[:, 512 * b:512 * b + C]

    sent = [0]

    def send(out, in_, rsem, dst, r):
        order("G", r, [])
        rid, pid, _s = topo.addr(dst)
        g.remote_dma(out, in_, T.sem[rsem], T.sem.sent, pid, rid, topo.mask(core, dst))
        sent[0] += len(topo.engines(core, dst))

    spare = []

    def later(f, *a, **k): spare.append(lambda: f(*a, **k))

    def fill(n=1):
        for _i in range(n):
            if spare: spare.pop(0)()

    partner = [T.cores[rank ^ s] for s in STEP]
    relay = [relay_of(T, topo, rank, s) for s in STEP]
    theirs = [relay_of(T, topo, rank ^ s, s) for s in STEP]

    load("Y", T.sei[:, :], T.se[:, :], "sei", "lse")
    load("S", T.ub[:, :], T.u[:, :], "ub", "lu")
    load("Y", T.x0[:, :], T.x[:, :], "x0", "lx")
    load("S", T.wq[:, :].bitcast(dt.uint8), T.wc[:, :], "wq", "lwc")
    load("Y", T.wqs[:, :], T.ws[:, :], "wqs", "lws")
    load("S", T.vb[:, :], T.v[:, :], "vb", "lv")

    LS = ["ls31", "ls8", "ls7", "ls6", "ls5", "ls4"]
    E0 = ["e0.%d" % j for j in range(4)]
    FC = ["fc%d" % j for j in range(10)]
    ZZ = ["zz%d" % j for j in range(5)]
    op("G", lambda e: e.iota(T.pi[:, :], [[0, 1]], 0, 1), [], ["pi"])
    iota(T.i512[:, 0:C], [[1, C]], 0, 0, ["i512"])
    iota(T.i16[:, :], [[0, 20], [1, 16]], 0, 0, ["i16"])
    iota(T.i512[:, C:512], [[1, 512 - C]], C, 0, ["i512b"])
    vset(T.idt[:, :], 0.5, ["idt"])
    vset(T.yt[:, :], 0.0, ["yt0"])
    vset(T.ls[:, :], 0, LS)
    vts(T.li[:, :], T.pi[:, :], 15, None, A.bitwise_and, None, ["pi"], ["li"])
    vset(T.m4[:, :], 0.0, ["m0", "m1", "m2", "m3"])
    vcp(T.lf[:, :], T.li[:, :], ["li"], ["lf"])
    for j in range(4):
        vts(T.x4[:, j:j + 1], T.li[:, :], 8 >> j, None, A.bitwise_and, None, ["li"], ["x4%d" % j])
    vts(T.tr[:, :], T.lf[:, :], 0.0, 640.0, A.is_equal, A.mult, ["lf"], ["tr"])
    for j in range(4):
        vts(T.bo[:, j:j + 1], T.x4[:, j:j + 1], 1.0 / (8 >> j), None, A.mult, None, ["x4%d" % j], ["bo%d" % j])
    vset(T.ma2[:, 240:256], 2.0, ["ma2b"])
    vcp(T.wo[:, 0:1], T.bo[:, 0:1], ["bo0"], ["wo0"])
    vset(T.pp[:, 40:41], 0.0, ["pp0"])
    vset(T.cs[:, 40:41], 0.0, ["cs0"])
    vts(T.fl0[:, :], T.lf[:, :], 0.0, None, A.is_equal, None, ["lf"], ["fl0"])
    vts(T.nd[:, :], T.i16[:, 0:16], T.lf[:, 0:1], None, A.subtract, None, ["i16", "lf"], ["nd"])
    vts(T.ma1[:, :], T.i16[:, :], T.lf[:, 0:1], None, A.is_equal, None, ["i16", "lf"], ["ma1"])
    act(T.dd[:, 0:640:2], T.i512[:, 0:C], ["i512"], ["dd"])
    act(T.dd[:, 1:640:2], T.i512[:, 0:C], ["i512"], ["dd1"])
    act(T.d0r[:, :], T.i16[:, :], ["i16"], ["d0r"], F.Sign)
    for b in range(4):
        act(T.eb[:, 512 * b:512 * b + 512], T.i512[:, :], ["i512", "i512b"], ["eb%d" % b], scale=0.0)
    op("G", lambda e: e.affine_select(T.idt[:, :], T.idt[:, :], [[-1, 128]], A.is_equal, 0.0, 0, 1), ["idt"], ["idt"])
    iota(T.zz[:, 1:16:2], [[0, 8]], 1, 0, ["zz0"])
    iota(T.zz[:, 2:16:4], [[0, 4]], 2, 0, ["zz1"])
    iota(T.zz[:, 4:16:8], [[0, 2]], 4, 0, ["zz2"])
    iota(T.zz[:, 8:9], [[0, 1]], 8, 0, ["zz3"])
    iota(T.zz[:, 0:1], [[0, 1]], 16, 0, ["zz4"])
    iota(T.i8[:, :], [[0, 8], [1, 4]], 0, 0, ["i8"])
    iota(T.fc[:, 0:32:4], [[0, 8]], 239, 0, ["fc0"])
    iota(T.fc[:, 1:32:4], [[0, 4], [16, 2]], 207, 0, ["fc1"])
    iota(T.fc[:, 2:32:4], [[0, 2], [16, 4]], 143, 0, ["fc2"])
    iota(T.fc[:, 3:32:4], [[16, 8]], 15, 0, ["fc3"])
    iota(T.fc[:, 32:40], [[4, 8]], 3, 0, ["fc4"])
    iota(T.fc[:, 40:48], [[1, 8]], 32, 0, ["fc5"])
    iota(T.fc[:, 48:56], [[4, 8]], 2, 0, ["fc6"])
    iota(T.fc[:, 56:60], [[4, 4]], 1, 0, ["fc7"])
    iota(T.fc[:, 60:62], [[4, 2]], 0, 0, ["fc8"])
    iota(T.fc[:, 62:64], [[1, 2]], 40, 0, ["fc9"])
    iota(T.e0[:, 0:32:4], [[0, 4], [16, 2]], -8, 0, ["e0.0"])
    iota(T.e0[:, 1:32:4], [[0, 2], [8, 2], [0, 2]], -4, 0, ["e0.1"])
    iota(T.e0[:, 2:32:4], [[4, 2], [0, 4]], -2, 0, ["e0.2"])
    iota(T.e0[:, 3:32:4], [[0, 8]], -1, 0, ["e0.3"])
    iota(T.ji[:, :], [[16, 32]], 320, 1, ["ji"])
    act(T.m4[:, 2:3], T.bo[:, 3:4], ["bo3"], ["m2"])
    act(T.m4[:, 1:2], T.bo[:, 2:3], ["bo2", "bo3"], ["m1"], F.Sign, bias=T.bo[:, 3:4])
    act(T.ini[:, :], T.fl0[:, :], ["fl0"], ["ini"], scale=-256.0)
    act(T.m4[:, 0:1], T.bo[:, 1:2], ["bo1", "m1"], ["m0"], F.Sign, bias=T.m4[:, 1:2])
    act(T.subl[:, :], T.lf[:, :], ["lf"], ["subl"], F.Identity, bias=15360.0, scale=-1024.0)
    act(T.ad[:, :], T.nd[:, :], ["nd"], ["ad"], F.Abs, bias=0.5, scale=-1.0)
    act(T.ma2[:, 0:240], T.ma1[:, 0:240], ["ma1"], ["ma2"], scale=2.0)
    act(T.d0l[:, :], T.ma1[:, :], ["ma1"], ["d0l"], F.Identity, bias=1024.0, scale=-66560.0)
    act(T.d0t[:, :], T.i8[:, :], ["i8"], ["d0t"], F.Sign)
    for b in range(4):
        act(T.eb[:, 512 * b + b:512 * b + 512:4], T.idt[:, :], ["idt"], ["eb%d" % b])

    vts(T.ofl[:, 0:1], T.sei[:, 0:1], T.tr[:, 0:1], None, A.add, None, ["sei", "tr"], ["ofl0"])
    vcp(T.ofl[:, 1:20], T.sei[:, 1:20], ["sei"], ["ofl"])
    vcp(T.dd[:, 0:656].indirect(T.ofl[:, 0:20]), T.i512[:, 0:C], ["ofl", "ofl0", "i512"], ["dd", "dd1"])
    later(vcp, T.ull[:, :], T.i512[:, 0:128:16], ["i512"], ["ull"])
    later(vts, T.ai[:, :], T.sei[:, :], 1, None, A.arith_shift_right, None, ["sei"], ["ai"])
    later(vts, T.sg[:, :], T.nd[:, :], 0.0, 0.5, A.is_le, A.subtract, ["nd"], ["sg"])
    later(vcp, T.parl[:, :], T.ai[:, :], ["ai"], ["parl"])
    later(vtt, T.an[:, :], T.ad[:, :], T.zz[:, :], A.is_lt, ["ad"] + ZZ, ["an"])
    later(vtt, T.oh[:, 0:3], T.m4[:, 0:3], T.m4[:, 1:4], A.subtract, ["m0", "m1", "m2", "m3"], ["oh"])
    later(vtt, T.w1[:, :], T.sg[:, :], T.zz[:, :], A.mult, ["sg"] + ZZ, ["w1"])
    later(vset, T.an[:, 0:1], 0.0, ["an"])
    later(vtt, T.zl[:, :], T.zz[:, :], T.ma1[:, 0:16], A.mult, ZZ + ["ma1"], ["zl"])
    later(vtt, T.w2[:, :], T.w1[:, :], T.an[:, :], A.mult, ["w1", "an"], ["w2"])
    later(vred, T.zr[:, :], T.zl[:, :], ["zl"], ["zr"])
    later(act, T.wt0[:, :], T.w2[:, :], ["w2"], ["wt0"], scale=32.0)
    later(vts, T.tm[:, :], T.zz[:, :], T.zr[:, 0:1], None, A.is_gt, None, ZZ + ["zr"], ["tm"])
    later(vtt, T.fm[:, :], T.fc[:, :], T.ma1[:, 0:64], A.mult, FC + ["ma1"], ["fm"])
    later(vtt, T.yo[:, 0:3], T.yt[:, 1:4], T.oh[:, 0:3], A.mult, ["oh", "yt1", "yt2", "yt3"], ["yo"])
    later(vscan, T.fs[:, :], T.d0r[:, 0:64], T.fm[:, :], 0.0, A.mult, A.add, ["fm", "d0r"], ["fs"])
    later(vred, T.yo[:, 4:5], T.yo[:, 0:3], ["yo"], ["yo4"])
    later(vcp, T.tl[:, 0:4], T.fs[:, 15:64:16], ["fs"], ["tl"])
    later(vcp, T.ls[:, 31:32], T.yo[:, 4:5], ["yo4"], ["ls31"])
    later(vtt, T.wm0[:, :], T.wt0[:, :], T.tm[:, :], A.mult, ["wt0", "tm"], ["wm0"])

    for j in range(4):
        vtt(T.g16[:, 16 * j:16 * j + 16], T.dd[:, 0:640].indirect(T.wo[:, 2 * j:2 * j + 1]), T.ma1[:, 0:16], A.mult,
            ["dd", "dd1", "wo%d" % j, "ma1"], ["g16%d" % j])
        fill()
        vred(T.yt[:, j + 1:j + 2], T.g16[:, 16 * j:16 * j + 16], ["g16%d" % j], ["yt%d" % (j + 1)])
        fill()
        y = T.yt[:, j + 1:j + 2]
        if j < 3:
            vts(T.wo[:, 2 * j + 2:2 * j + 3], y, 2.0, T.bo[:, j + 1:j + 2], A.mult, A.add, ["yt%d" % (j + 1), "bo%d" % (j + 1)], ["wo%d" % (j + 1)])
        else:
            vts(T.wv[:, 0:1], y, 2.0, None, A.mult, None, ["yt4"], ["wv0"])
            vts(T.wv[:, 1:2], y, 2.0, 1.0, A.mult, A.add, ["yt4"], ["wv1"])
            vcp(T.ls[:, 30:31], y, ["yt4"], ["ls4"])
        fill()

    for n, s1, b, o, o1 in ((1, 28, "ls5", 0, 2), (2, 24, "ls6", 2, 6), (4, 16, "ls7", 6, 14), (8, 0, "ls8", 14, 0)):
        k, h = 32 * n, 32 * (n - 1)
        vtt(T.gg[:, h:h + k], T.dd[:, 0:640].indirect(T.wv[:, o:o + 2 * n]), T.ma1[:, 0:k], A.mult, ["dd", "dd1", "wv0", "wv1", "ma1"], [b + "g"])
        if n == 1:
            quant(T.uq[:, :], T.us[:, :], T.ub[:, :], ["ub"], ["uq"])
        else: fill()
        vscan(T.gs[:, h:h + k], T.d0r[:, 0:k], T.gg[:, h:h + k], 0.0, A.mult, A.add, [b + "g", "d0r"], [b + "s"])
        if n == 1:
            vcp(T.ur[:, 0:128].bitcast(dt.uint32), T.uq[:, 0:128].bitcast(dt.uint32).indirect(T.ull[:, 0:8]), ["uq", "ull"], ["ur"])
            act(T.urs[:, 0:128], T.us[:, 0:128].indirect(T.ull[:, 0:8]), ["uq", "ull"], ["urs"])
        elif n == 2:
            quant(T.q0[:, 0:C], T.qs0[:, 0:C], T.x0[:, 0:1280], ["x0"], ["q0.0"])
        else: fill()
        y = T.gs[:, h + 15:h + k:16]
        if n < 8:
            vts(T.wv[:, o1:o1 + 2 * n], y, 2.0, None, A.mult, None, [b + "s"], ["wv0"])
            vts(T.wv[:, o1 + 2 * n:o1 + 4 * n], y, 2.0, 1.0, A.mult, A.add, [b + "s"], ["wv1"])
        vcp(T.ls[:, s1:s1 + 2 * n], y, [b + "s"], [b])
        fill()
    fill(len(spare))

    def labels(k):
        send(T.ll[:, 32 * k:32 * k + 32], T.ls[:, 0:32], "lb%d" % k, relay[k] or partner[k], LS)

    labels(0)

    later(vcp, T.yf[:, :], T.ls[:, :], LS, ["yf"])
    later(vts, T.tls[:, 0:2], T.fs[:, 15:32:16], 0.0625, 15.0625, A.mult, A.add, ["fs"], ["tls"])
    later(vtt, T.eqp[:, :], T.yt[:, 0:4], T.yt[:, 1:5], A.is_equal, ["yt0", "yt1", "yt2", "yt3", "yt4"], ["eqp"])
    later(vtt, T.y32[:, :], T.yf[:, :], T.ji[:, :], A.subtract, ["yf", "ji"], ["y32"])
    later(vcp, T.lab[:, :], T.yf[:, :].indirect(T.tls[:, 0:2]), ["yf", "tls"], ["lab"])
    later(vtt, T.eqm[:, :], T.eqp[:, :], T.m4[:, :], A.mult, ["eqp", "m0", "m1", "m2", "m3"], ["eqm"])
    later(vred, T.cb[:, :], T.eqp[:, :], ["eqp"], ["cb"])
    later(vtt, T.eqv[:, 0:31], T.lab[:, 1:32], T.lab[:, 0:31], A.is_equal, ["lab"], ["eqv"])
    later(vred, T.ct[:, :], T.eqm[:, :], ["eqm"], ["ct"])
    later(vtt, T.eqr[:, :], T.lab[:, 3:32:4], T.yf[:, 8:16], A.is_equal, ["lab", "yf"], ["eqr"])
    later(vtt, T.eqv[:, 3:32:4], T.lab[:, 3:32:4], T.yf[:, 0:8], A.is_equal, ["lab", "yf"], ["eqv"])
    later(vts, T.cs[:, 41:42], T.ct[:, :], T.cb[:, 0:1], T.fl0[:, 0:1], A.subtract, A.add, ["ct", "cb", "fl0"], ["cst"])
    later(vscan, T.cs[:, 0:32], T.d0t[:, :], T.eqv[:, :], 0.0, A.mult, A.add, ["eqv", "d0t"], ["cs"])
    later(vtt, T.cs[:, 32:40], T.cs[:, 2:32:4], T.eqr[:, :], A.add, ["cs", "eqr"], ["csr"])
    later(vts, T.z32[:, :], T.cs[:, 0:42].indirect(T.tl[:, 2:4]), T.cb[:, 0:1], 0.0, A.add, A.is_equal, ["cs", "csr", "cst", "cs0", "cb", "tl"], ["z32"])
    later(vtt, T.zy[:, :], T.z32[:, :], T.y32[:, :], A.mult, ["z32", "y32"], ["zy"])
    later(vtt, T.o32[:, :], T.zy[:, :], T.ji[:, :], A.add, ["zy", "ji"], ["o32"])
    later(vcp, T.ol[:, :], T.o32[:, :], ["o32"], ["ol"])

    for r in range(3):
        q, qs, qt = T["q%d" % (r % 2)], T["qs%d" % (r % 2)], "q%d" % (r % 2)
        Q, QS = q[:, 0:C], qs[:, 0:C]
        parts = PARTS if r else [(0, C)]
        qp = ["%s.%d" % (qt, i) for i in range(len(parts))]
        wb, fb, ab = [[1, 2, 3, 4], [6, 7, 0, 5]], [[6, 7, 0, 5], [1, 2, 3, 4]][len(parts) - 1], [[1, 2, 3, 4], [6, 7, 0, 5]][len(parts) - 1]
        far = relay[r] is not None
        hq, hs, lq, lqs = T["hq%d" % r], T["hs%d" % r], T["lq%d" % r], T["lqs%d" % r]

        def scores(i):
            c0, c1 = parts[i]
            mm(5 * i, T.ur[:, 0:128], T.urs[:, 0:128], q[:, c0:c1], qs[:, c0:c1], [qp[i], "ur", "urs"], c1 - c0)

        def layer(i):
            c0, c1 = parts[i]
            for b in range(4):
                mm(wb[i][b], T.wq[:, 128 * b:128 * b + 128], T.wqs[:, 128 * b:128 * b + 128], q[:, c0:c1], qs[:, c0:c1], [qp[i], "wq", "wqs"], c1 - c0)
            for b in range(4):
                k = wb[i][b]
                act(T.hb[:, 4 * c0 + b:4 * c1:4], T.ps[:, 512 * k:512 * k + c1 - c0], ["bank%d" % k], ["hb%d.%d" % (i, b)], scale=0.03125)

        def pack(c0, c1, ii, t):
            quant(hq[:, c0:c1], hs[:, c0:c1], T.hb[:, 4 * c0:4 * c1], ["hb%d.%d" % (i, b) for i in ii for b in range(4)], [t])

        def signs(i):
            c0, c1 = parts[i]
            vts(T.tb[:, c0:c1], T.ps[:, 2560 * i:2560 * i + c1 - c0], 0.0, 0.5, A.is_ge, A.subtract, ["bank%d" % (5 * i)], ["tb%d" % i])

        if far:
            c0, c1 = parts[0]
            layer(0)
            scores(0)
            scores(1)
            pack(c0, c1, [0], "hqa")
            send(hq[:, c0:c1].bitcast(dt.uint8), hq[:, c0:c1].bitcast(dt.uint8), "hand", relay[r], ["hqa"])
            send(lqs[:, c0:c1], hs[:, c0:c1], "sra", partner[r], ["hqa"])
        else:
            scores(0)
            layer(0)
            if r: scores(1)
        for i in range(len(parts)): signs(i)
        if r: layer(1)
        fill()
        vtt(T.mg[:, :], T.tb[:, 0:C].indirect(T.ls[:, 16:32]), T.ma2[:, 0:256], A.mult, ["tb0", "tb1", "ma2", "ma2b"] + LS, ["mg"])
        fill()
        vscan(T.sc[:, :], T.d0r[:, 0:240], T.mg[:, 0:240], 0.0, A.mult, A.add, ["mg", "d0r"], ["sc"])
        o, n = r % 2, 1 - r % 2
        vtt(T["wt%d" % n][:, :], T.mg[:, 240:256], T["wt%d" % o][:, :], A.mult, ["mg", "wt%d" % o], ["wt%d" % n])
        eo, en, te, tn = (T.e0, T.e1, E0, ["e1"]) if r % 2 == 0 else (T.e1, T.e0, ["e1"], E0)
        vtt(en[:, :], T.sc[:, 0:240].indirect(T.tl[:, 0:2]), eo[:, :], A.mult, ["sc", "tl"] + te, tn)
        vtt(T["wm%d" % n][:, :], T.mg[:, 240:256], T["wm%d" % o][:, :], A.mult, ["mg", "wm%d" % o], ["wm%d" % n])
        vred(T.ba[:, :], T["wt%d" % n][:, :], ["wt%d" % n], ["ba"])
        vscan(T.pp[:, 0:32], T.d0t[:, :], en[:, :], 0.0, A.mult, A.add, tn + ["d0t"], ["pp"])
        vred(T.bt[:, :], T["wm%d" % n][:, :], ["wm%d" % n], ["bt"])
        vtt(T.pp[:, 32:40], T.pp[:, 2:32:4], en[:, 3:32:4], A.subtract, ["pp"] + tn, ["ppr"])
        vts(T.pp[:, 41:42], T.bt[:, :], T.ba[:, 0:1], T.ini[:, 0:1], A.subtract, A.add, ["bt", "ba", "ini"], ["ppt"])
        pl, pa = T.pl[:, 32 * r:32 * r + 32], T.pa[:, 32 * r:32 * r + 32]
        vts(pl, T.pp[:, 0:42].indirect(T.tl[:, 2:4]), T.ba[:, 0:1], 256.0, A.add, A.add, ["pp", "ppr", "ppt", "pp0", "ba", "tl"], ["pl%d" % r])
        send(pa, pl, "pr%d" % r, partner[r], ["pl%d" % r])
        fill()
        c0, c1 = parts[1] if far else (0, C)
        pack(c0, c1, [1] if far else range(len(parts)), "hq%d" % r)
        send(lq[:, c0:c1].bitcast(dt.uint8), hq[:, c0:c1].bitcast(dt.uint8), "cr%d" % r, partner[r], ["hq%d" % r])
        send(lqs[:, c0:c1], hs[:, c0:c1], "sr%d" % r, partner[r], ["hq%d" % r])
        fill()
        if r == 0:
            labels(1)
            labels(2)
            quant(T.eq[:, :], T.es[:, :], T.eb[:, :], ["eb0", "eb1", "eb2", "eb3"], ["eq"])
        for b in range(4):
            mm(fb[b], T.eq[:, 128 * b:128 * b + 128], T.es[:, 128 * b:128 * b + 128], Q, QS, qp + ["eq"])
        act(T.prep[:, :], T.i512[:, :].indirect(pl), ["i512", "i512b", "pl%d" % r], ["prep"])
        if r == 0:
            for b in range(4):
                act(T.fw[:, C * b:C * b + C], bank(fb[b]), ["bank%d" % fb[b]], ["fw%d" % b])
            fill(len(spare))
            vcp(T.at[:, 0:960].indirect(T.ol[:, 0:32]), T.i512[:, :], ["ol", "i512", "i512b"], ["at"])
            vscan(T.als[:, :], T.d0l[:, :], T.at[:, 0:C], 0.0, A.add, A.max, ["at", "d0l"], ["als"])
            vts(T.al[:, :], T.als[:, 15:C:16], T.subl[:, 0:1], None, A.subtract, None, ["als", "subl"], ["al"])
            lastw["ll0"] = ("lb0", len(topo.engines(core, partner[0])))
            act(T.lr[:, 0:512], T.i512[:, 0:C].indirect(T.ll[:, 0:32]), ["i512", "ll0"], ["lr0"])
            for b in range(2):
                act(T.fg[:, C * b:C * b + C], T.fw[:, C * b:C * b + C].indirect(T.parl[:, 0:20]), ["fw%d" % b, "parl"], ["fg%d" % b])
        act(T.brep[:, :], T.prep[:, :].indirect(T.al[:, 0:20]), ["prep", "al"], ["brep"])
        if r:
            for b in range(4):
                vcp(T.fw[:, C * b:C * b + C], bank(fb[b]), ["bank%d" % fb[b]], ["fw%d" % b])
        if r == 1:
            quant(T.vq[:, :], T.vs[:, :], T.vb[:, :], ["vb"], ["vq"])
        for b in range(0 if r else 2, 4):
            act(T.fg[:, C * b:C * b + C], T.fw[:, C * b:C * b + C].indirect(T.parl[:, 0:20]), ["fw%d" % b, "parl"], ["fg%d" % b])
        k = len(topo.engines(core, partner[r]))
        lastw["pa%d" % r], lastw["lq%d" % r], lastw["lqs%d" % r] = ("pr%d" % r, k), ("cr%d" % r, k), ("sr%d" % r, k)
        zt = (T.zt[:, :].indirect(pa), T.lr[:, 512 * r:512 * r + 512], ["pa%d" % r, "lr%d" % r], ["zt"])
        if r == 0: vcp(*zt)
        vscan(T.bsc[:, :], T.d0l[:, :], T.brep[:, :], 0.0, A.add, A.max, ["brep", "d0l"], ["bsc"])
        vts(T.bl[:, :], T.bsc[:, 15:C:16], T.subl[:, 0:1], None, A.subtract, None, ["bsc", "subl"], ["bl"])
        if r: vcp(*zt)
        vcp(T.mr[:, :], T.zt[:, :].indirect(T.bl[:, 0:20]), ["zt", "bl"], ["mr"])
        vscan(T.msc[:, :], T.d0l[:, :], T.mr[:, :], 0.0, A.add, A.max, ["mr", "d0l"], ["msc"])
        vts(T.ml[:, :], T.msc[:, 15:C:16], T.subl[:, 0:1], None, A.subtract, None, ["msc", "subl"], ["ml"])
        if r == 2:
            store("Y", T.im[:, :], T.mr[0:128:16, :], ["mr"])
        runs = [(0, C, ab, ["lq%d" % r, "lqs%d" % r])]
        if far:
            lastw["lqa"], lastw["lqsa"] = ("handed", len(topo.engines(theirs[r], core))), ("sra", k)
            runs = [parts[0] + ([1, 2, 3, 4], ["lqa", "lqsa"]), parts[1] + (ab, ["lq%d" % r, "lqs%d" % r])]
        for c0, c1, bb, tt in runs:
            for b in range(4):
                mm(bb[b], T.eq[:, 128 * b:128 * b + 128], T.es[:, 128 * b:128 * b + 128], lq[:, c0:c1], lqs[:, c0:c1], tt + ["eq"], c1 - c0)
        for j, (c0, c1, bb, tt) in enumerate(runs):
            for b in range(4):
                act(T.aw[:, C * b + c0:C * b + c1], T.ps[:, 512 * bb[b]:512 * bb[b] + c1 - c0], ["bank%d" % bb[b]], ["aw%d.%d" % (j, b)])
        n = r + 1
        for i, (c0, c1) in enumerate(PARTS):
            for b in range(4):
                vtt(T.xr[:, 4 * c0 + b:4 * c1:4], T.aw[:, C * b:C * b + C].indirect(T.ml[:, c0 // 16:c1 // 16]), T.fg[:, C * b + c0:C * b + c1], A.add,
                    ["aw0.%d" % b, "aw1.%d" % b, "ml", "fg%d" % b], ["xr%d.%d" % (i, b)])
            quant(T["q%d" % (n % 2)][:, c0:c1], T["qs%d" % (n % 2)][:, c0:c1], T.xr[:, 4 * c0:4 * c1], ["xr%d.%d" % (i, b) for b in range(4)], ["q%d.%d" % (n % 2, i)])
        if r < 2:
            lastw["ll%d" % n] = ("lb%d" % n, len(topo.engines(theirs[n] or partner[n], core)))
            act(T.lr[:, 512 * n:512 * n + 512], T.i512[:, 0:C].indirect(T.ll[:, 32 * n:32 * n + 32]), ["i512", "ll%d" % n], ["lr%d" % n])

    for i, (c0, c1) in enumerate(PARTS):
        t = "q1.%d" % i
        mm(5 * i, T.vq[:, 0:128], T.vs[:, 0:128], T.q1[:, c0:c1], T.qs1[:, c0:c1], [t, "vq"], c1 - c0)
        vcp(T.ysb[:, c0:c1], T.ps[:, 2560 * i:2560 * i + c1 - c0], ["bank%d" % (5 * i)], ["ysb%d" % i])
        store("Y", T.oc[:, 4 * c0:4 * c1], T.q1[:, c0:c1].bitcast(dt.uint8), [t])
        for k in range(4):
            store("S", T.osc[4 * k:4 * k + 4, c0:c1], T.qs1[32 * k:32 * k + 4, c0:c1], [t])
        store("Y", T.y[:, c0:c1], T.ysb[:, c0:c1], ["ysb%d" % i])
    for k in ("V", "S", "T", "G"):
        wait("G", ("c" + k, cnt[k]))
    g.wait_ge(T.sem.stored, stores[0])
    g.wait_ge(T.sem.sent, sent[0])
